import numpy as np
import ml_dtypes


def mxq(x, axis, fmt="e4m3"):
    dtype, down = {"e4m3": (ml_dtypes.float8_e4m3fn, 7), "e5m2": (ml_dtypes.float8_e5m2, 14)}[fmt]
    v = np.moveaxis(np.asarray(x, np.float32).astype(ml_dtypes.bfloat16).astype(np.float64), axis, -1)
    blocks = v.reshape(v.shape[:-1] + (-1, 32))
    amax = np.abs(blocks).max(-1, keepdims=True)
    byte = np.maximum(np.where(amax > 0, np.frexp(amax)[1] - 1 + 127, 0) - down, 1)
    scale = np.exp2(byte - 127.0)
    codes = (blocks / scale).astype(np.float32).astype(dtype).astype(np.float64)
    return np.moveaxis((codes * scale).reshape(v.shape), -1, axis)


WIDE = False


def mx_kscale(k):
    if not WIDE:
        return np.ones(k)
    levels = np.array([24, -24, 12, -12, 0])
    if k % 512:
        return np.exp2(np.random.permutation(np.resize(levels, k // 32))).repeat(32)
    a = np.empty((k // 512, 16))
    for p in range(k // 512):
        a[p, :8] = np.random.permutation(np.resize(levels, 8))
        for g in range(8):
            far = levels[np.abs(levels - a[p, g]) >= 10]
            a[p, g + 8] = far[np.random.randint(len(far))]
    return np.exp2(a.ravel()).repeat(32)


def f64(x):
    return np.asarray(x).astype(np.float64)


def striped(idx):
    return np.tile(idx.reshape(-1, 16).T, (8, 1)).astype(np.uint16)


def unstriped(offs):
    return offs[:16].T.reshape(-1).astype(np.int64)


E2M1 = np.array([0.0, 0.5, 1.0, 1.5, 2.0, 3.0, 4.0, 6.0, -0.0, -0.5, -1.0, -1.5, -2.0, -3.0, -4.0, -6.0])


def pack_weight(w, fmt):
    k, n = w.shape
    w = f64(np.asarray(w, np.float32).astype(ml_dtypes.bfloat16)).reshape(k // 32, 32, n)
    amax = np.abs(w).max(1)
    if fmt == "e4m3":
        byte = np.frexp(amax)[1] - 1 + 127 - 7
    else:
        mant, ex = np.frexp(amax / 6.0)
        byte = np.where(mant > 0.5, ex, ex - 1) + 127
    byte = np.clip(np.where(amax > 0, byte, 1), 1, 254)
    scaled = (w * np.exp2(127.0 - byte)[:, None, :]).reshape(k, n).astype(np.float32)
    by_word = np.ascontiguousarray(scaled.reshape(k // 512, 128, 4, n).transpose(0, 1, 3, 2))
    if fmt == "e4m3":
        words = by_word.astype(ml_dtypes.float8_e4m3fn).view(np.uint8)
    else:
        c = by_word.astype(ml_dtypes.float4_e2m1fn).view(np.uint8) & 0xF
        words = (c[..., 0::2] | (c[..., 1::2] << 4)).reshape(k // 512, 128, 2 * n)
    return np.ascontiguousarray(words), np.ascontiguousarray(byte.astype(np.uint8).reshape(k // 512, 16, n))


def unpack_weight(words, scales, fmt):
    g, _, n = scales.shape
    words = np.ascontiguousarray(words).reshape(g, 128, n, -1)
    if fmt == "e4m3":
        vals = words.view(ml_dtypes.float8_e4m3fn).astype(np.float64)
    else:
        nib = np.empty((g, 128, n, 4), np.uint8)
        nib[..., 0::2] = words & 0xF
        nib[..., 1::2] = words >> 4
        vals = E2M1[nib]
    vals = vals * np.repeat(np.exp2(scales.astype(np.float64) - 127.0), 8, axis=1)[..., None]
    return vals.transpose(0, 1, 3, 2).reshape(g * 512, n)


K, R, N, T, J = 1024, 1024, 256, 1024, 512


def setup_inputs():
    n = np.random.standard_normal
    s = mx_kscale(K)[:, None]
    u = mx_kscale(R)[:, None]
    wb = 0.7 * n((K, N)) / np.sqrt(K) / s
    p_tab = pack_weight(n((K, T)) * s, "e4m3")
    p_wb8 = pack_weight(wb[:512], "e4m3")
    p_wb4 = pack_weight(wb[512:], "e2m1")
    p_dn = pack_weight(n((K, R)) / np.sqrt(K) / s * u.T, "e4m3")
    return {
        "tab_words": p_tab[0],
        "tab_scales": p_tab[1],
        "wb8_words": p_wb8[0],
        "wb8_scales": p_wb8[1],
        "wb4_words": p_wb4[0],
        "wb4_scales": p_wb4[1],
        "dn_words": p_dn[0],
        "dn_scales": p_dn[1],
        "upw": (2.0 * n((R, N)) / np.sqrt(R) / u).astype(np.float32),
        "x0T": (n((N, T))).astype(np.float32),
        "b": (0.3 * n(N)).astype(np.float32),
        "offs": striped(np.random.permutation(T)[:J]),
    }


def reference(tab_words, tab_scales, wb8_words, wb8_scales, wb4_words, wb4_scales, dn_words, dn_scales, upw, x0T, b, offs):
    idx = unstriped(offs)
    tab_ = unpack_weight(tab_words, tab_scales, "e4m3")[:, idx]
    wb8_ = unpack_weight(wb8_words, wb8_scales, "e4m3")
    wb4_ = unpack_weight(wb4_words, wb4_scales, "e2m1")
    dn_ = unpack_weight(dn_words, dn_scales, "e4m3")
    hs = dn_.T @ tab_
    h = np.maximum(hs, 0.0)
    h_ = mxq(h, 0, "e4m3")
    upw_ = mxq(f64(upw), 0, "e4m3")
    y = wb8_.T @ tab_[:512] + wb4_.T @ tab_[512:] + upw_.T @ h_
    return f64(x0T)[:, idx] * (y + f64(b)[:, None]) + f64(x0T)[:, idx]

@@ -1,0 +1,233 @@
+from contextlib import ExitStack
+
+import concourse.mybir as mybir
+
+K, R, N, T, J = 1024, 1024, 256, 1024, 512
+FLOPS = 2 * J * (K * R + K * N + R * N)
+
+F32 = mybir.dt.float32
+BF16 = mybir.dt.bfloat16
+I32 = mybir.dt.int32
+U32 = mybir.dt.uint32
+U16 = mybir.dt.uint16
+U8 = mybir.dt.uint8
+FP8X4 = mybir.dt.float8_e4m3fn_x4
+FP4X4 = mybir.dt.float4_e2m1fn_x4
+ACT = mybir.ActivationFunctionType
+ALU = mybir.AluOpType
+
+P = 128
+PACK = 4
+K_PASS = P * PACK
+HALF = J // 2
+QUARTER = J // 4
+QUADS = 4
+
+
+def tile_list_xcross_mix_relu_kernel(
+    tc, tab_words, tab_scales, wb8_words, wb8_scales, wb4_words, wb4_scales, dn_words, dn_scales, upw, x0T, b, offs, out
+):
+    nc = tc.nc
+    with ExitStack() as ctx:
+        lists = ctx.enter_context(tc.tile_pool(name="lists", bufs=1))
+        keep = ctx.enter_context(tc.tile_pool(name="keep", bufs=1))
+        psum_h = ctx.enter_context(tc.psum_pool(name="psum_h", bufs=6))
+        psum_y = ctx.enter_context(tc.psum_pool(name="psum_y", bufs=1))
+
+        def held(name, shape, dtype):
+            return keep.tile(shape, dtype, name=name, align_bytes=64)
+
+        offsets = lists.tile([P, J // 16], U16, name="offsets")
+        half_list = [offsets[:, h * HALF // 16 : (h + 1) * HALF // 16] for h in range(2)]
+
+        tab_plane = held("tab_plane", [P, T], U8)
+        dn_plane_raw = held("dn_plane_raw", [P, R], U8)
+        wb8_plane = held("wb8_plane", [P, N], U8)
+        wb4_plane = held("wb4_plane", [P, N], U8)
+        low_plane = held("low_plane", [P, J], U8)
+        nc.vector.memset(tab_plane[:].bitcast(I32), 0)
+        nc.vector.memset(dn_plane_raw[:].bitcast(I32), 0)
+        nc.vector.memset(wb8_plane[:].bitcast(I32), 0)
+        nc.vector.memset(wb4_plane[:].bitcast(I32), 0)
+        nc.vector.memset(low_plane[:].bitcast(I32), 0)
+
+        def load_scale_rows(queue, plane, scales, quad):
+            passes = scales.shape[0]
+            queue.dma_start(
+                out=plane[32 * quad : 32 * quad + 4 * passes, :].bitcast(I32),
+                in_=scales[:, 4 * quad : 4 * quad + 4, :].bitcast(I32),
+            )
+
+        def words_of(words, a):
+            return words[a].rearrange("p c i -> p (c i)").bitcast(I32)
+
+        tab_w = [held(f"tab_w{a}", [P, T], I32) for a in range(2)]
+        dn_raw0 = held("dn_raw0", [P, R], I32)
+        dn_raw1 = [held(f"dn_raw1_{c}", [P, K_PASS], I32) for c in range(2)]
+        x0 = [held(f"x0_{c}", [P, T], F32) for c in range(2)]
+        wb8_w = held("wb8_w", [P, N], I32)
+        wb4_w = held("wb4_w", [P, 2 * N], U8)
+        bias = held("bias", [P, 2], F32)
+        up_raw = [held(f"up_raw{c}", [P, PACK, N], F32) for c in range(2)]
+
+        nc.sync.dma_start(offsets[:], offs)
+        for quad in range(QUADS):
+            load_scale_rows(nc.scalar, tab_plane, tab_scales, quad)
+        for quad in range(QUADS):
+            load_scale_rows(nc.scalar, dn_plane_raw, dn_scales, quad)
+        with nc.allow_non_contiguous_dma(reason="one bias value a partition"):
+            nc.gpsimd.dma_start(out=bias[:], in_=b.rearrange("(c p) -> p c", p=P))
+        nc.sync.dma_start(out=tab_w[0][:], in_=words_of(tab_words, 0))
+        nc.sync.dma_start(out=dn_raw0[:], in_=words_of(dn_words, 0))
+        nc.sync.dma_start(out=tab_w[1][:], in_=words_of(tab_words, 1))
+        for c in range(2):
+            nc.sync.dma_start(out=dn_raw1[c][:], in_=words_of(dn_words, 1)[:, c * K_PASS : (c + 1) * K_PASS])
+        for c, (plane, scales) in enumerate(((wb8_plane, wb8_scales), (wb4_plane, wb4_scales))):
+            nc.sync.dma_start(out=x0[c][:], in_=x0T[c * P : (c + 1) * P, :])
+            for quad in range(QUADS):
+                load_scale_rows(nc.scalar, plane, scales, quad)
+        nc.sync.dma_start(out=wb8_w[:], in_=words_of(wb8_words, 0))
+        nc.sync.dma_start(out=wb4_w[:].bitcast(I32), in_=wb4_words[0].bitcast(I32))
+        for c in range(2):
+            rows = upw[c * K_PASS : (c + 1) * K_PASS, :].rearrange("(g t q) n -> t g q n", t=PACK, q=8)
+            for t in range(PACK):
+                nc.sync.dma_start(out=up_raw[c][:, t, :], in_=rows[t])
+
+        v_plane = held("v_plane", [P, J], U8)
+        v_w = [[held(f"v_w{a}_{h}", [P, HALF], U32) for h in range(2)] for a in range(2)]
+        dn_plane = held("dn_plane", [P, R], U8)
+        dn_w = [[held(f"dn_w{a}_{c}", [P, K_PASS], I32) for c in range(2)] for a in range(2)]
+
+        def gather_plane(h):
+            nc.vector.tensor_copy(v_plane[:, h * HALF : (h + 1) * HALF], tab_plane[:].indirect(half_list[h]))
+
+        def gather_words(a, h):
+            nc.vector.tensor_copy(v_w[a][h][:], tab_w[a][:].bitcast(U32).indirect(half_list[h]))
+
+        def order_words(a, c, raw):
+            nc.vector.tensor_copy(
+                out=dn_w[a][c][:].rearrange("p (t g q) -> p t g q", t=PACK, q=8),
+                in_=raw.rearrange("p (g t q) -> p t g q", t=PACK, q=8),
+            )
+
+        gather_plane(0)
+        gather_plane(1)
+        gather_words(0, 0)
+        nc.vector.tensor_copy(
+            out=dn_plane[:].bitcast(I32).rearrange("p (c t g w) -> p c t g w", c=2, t=PACK, w=2),
+            in_=dn_plane_raw[:].bitcast(I32).rearrange("p (c g t w) -> p c t g w", c=2, t=PACK, w=2),
+        )
+        order_words(0, 0, dn_raw0[:, 0:K_PASS])
+        order_words(0, 1, dn_raw0[:, K_PASS:R])
+        gather_words(1, 0)
+        order_words(1, 0, dn_raw1[0][:])
+        order_words(1, 1, dn_raw1[1][:])
+        gather_words(0, 1)
+        gather_words(1, 1)
+
+        nc.gpsimd.dma_start(out=low_plane[0:112, :].bitcast(I32), in_=v_plane[4:116, :].bitcast(I32))
+
+        bias1 = held("bias1", [P, 2], F32)
+        nc.scalar.activation(bias1[:], bias[:], ACT.Copy, bias=1.0)
+
+        x0_g = [held(f"x0_g{c}", [P, J], F32) for c in range(2)]
+        for c in range(2):
+            nc.vector.tensor_copy(x0_g[c][:], x0[c][:].indirect(offsets[:]))
+
+        def hs_passes(bank, a, c, h, s):
+            cols = slice(s * QUARTER, (s + 1) * QUARTER)
+            jcols = slice(h * HALF + s * QUARTER, h * HALF + (s + 1) * QUARTER)
+            for t in range(PACK):
+                nc.tensor.matmul_mx(
+                    out=bank[:, t, :],
+                    lhsT=dn_w[a][c][:, t * P : (t + 1) * P].bitcast(FP8X4),
+                    lhsT_scale=dn_plane[4 * a :, c * K_PASS + t * P : c * K_PASS + (t + 1) * P],
+                    rhs=v_w[a][h][:, cols].bitcast(FP8X4),
+                    rhs_scale=v_plane[4 * a :, jcols],
+                    start=(a == 0 and t == 0),
+                    stop=(a == 1 and t == PACK - 1),
+                )
+
+        h_w = {}
+        h_plane = {}
+        for h in range(2):
+            banks = {(c, s): psum_h.tile([P, PACK, QUARTER], F32, name="hs") for c in range(2) for s in range(2)}
+            if h == 0:
+                for (c, s), bank in banks.items():
+                    hs_passes(bank, 0, c, h, s)
+            for c in range(2):
+                h_bf = held(f"h_bf{h}_{c}", [P, HALF, PACK], BF16)
+                for s in range(2):
+                    if h == 1:
+                        hs_passes(banks[c, s], 0, c, h, s)
+                    hs_passes(banks[c, s], 1, c, h, s)
+                    nc.scalar.activation(
+                        h_bf[:, s * QUARTER : (s + 1) * QUARTER, :],
+                        banks[c, s][:].rearrange("p t j -> p j t"),
+                        ACT.Relu,
+                    )
+                h_w[h, c] = held(f"h_w{h}_{c}", [P, HALF], U32)
+                h_plane[h, c] = held(f"h_plane{h}_{c}", [P, HALF], U8)
+                nc.vector.quantize_mx(
+                    out=h_w[h, c][:].bitcast(FP8X4),
+                    scales=h_plane[h, c][:],
+                    in_=h_bf[:].rearrange("p j t -> p (j t)"),
+                )
+
+        up_w = []
+        up_plane = []
+        for c in range(2):
+            up_bf = held(f"up_bf{c}", [P, N, PACK], BF16)
+            dst = up_bf[:].rearrange("p (n i) t -> p n t i", i=4)
+            src = up_raw[c][:].rearrange("p t (n i) -> p n t i", i=4)
+            if c == 0:
+                nc.scalar.copy(dst, src)
+            else:
+                nc.vector.tensor_copy(dst, src)
+            up_w.append(held(f"up_w{c}", [P, N], U32))
+            up_plane.append(held(f"up_plane{c}", [P, N], U8))
+            nc.vector.quantize_mx(
+                out=up_w[c][:].bitcast(FP8X4), scales=up_plane[c][:], in_=up_bf[:].rearrange("p n t -> p (n t)")
+            )
+
+        for h in range(2):
+            y = psum_y.tile([P, 2, HALF], F32, name=f"y{h}")
+            jcols = slice(h * HALF, (h + 1) * HALF)
+            for m in range(2):
+                nc.tensor.matmul_mx(
+                    out=y[:, m, :],
+                    lhsT=wb8_w[:, m * P : (m + 1) * P].bitcast(FP8X4),
+                    lhsT_scale=wb8_plane[:, m * P : (m + 1) * P],
+                    rhs=v_w[0][h][:].bitcast(FP8X4),
+                    rhs_scale=v_plane[:, jcols],
+                    start=(m == 0),
+                    stop=False,
+                )
+            for m in range(2):
+                for s in range(2):
+                    nc.tensor.matmul_mx(
+                        out=y[:, m, s * QUARTER : (s + 1) * QUARTER],
+                        lhsT=wb4_w[:, 2 * m * P : 2 * (m + 1) * P].bitcast(FP4X4),
+                        lhsT_scale=wb4_plane[:, m * P : (m + 1) * P],
+                        rhs=v_w[1][h][:, s * QUARTER : (s + 1) * QUARTER].bitcast(FP8X4),
+                        rhs_scale=low_plane[:, h * HALF + s * QUARTER : h * HALF + (s + 1) * QUARTER],
+                        start=False,
+                        stop=False,
+                    )
+            for c in range(2):
+                for m in range(2):
+                    nc.tensor.matmul_mx(
+                        out=y[:, m, :],
+                        lhsT=up_w[c][:, m * P : (m + 1) * P].bitcast(FP8X4),
+                        lhsT_scale=up_plane[c][:, m * P : (m + 1) * P],
+                        rhs=h_w[h, c][:].bitcast(FP8X4),
+                        rhs_scale=h_plane[h, c][:],
+                        start=False,
+                        stop=(c == 1 and m == 1),
+                    )
+            for m in range(2):
+                res = held(f"res{h}_{m}", [P, HALF], F32)
+                nc.vector.scalar_tensor_tensor(
+                    out=res[:], in0=y[:, m, :], scalar=bias1[:, m : m + 1], in1=x0_g[m][:, jcols], op0=ALU.add, op1=ALU.mult
+                )
+                nc.sync.dma_start(out=out[m * P : (m + 1) * P, jcols], in_=res[:])

@@ -34,8 +34,8 @@ def tile_list_xcross_mix_relu_kernel(
         psum_h = ctx.enter_context(tc.psum_pool(name="psum_h", bufs=6))
         psum_y = ctx.enter_context(tc.psum_pool(name="psum_y", bufs=1))
 
-        def held(name, shape, dtype):
-            return keep.tile(shape, dtype, name=name, align_bytes=64)
+        def held(name, shape, dtype, tag=None):
+            return keep.tile(shape, dtype, name=name, tag=tag or name, align_bytes=64)
 
         offsets = lists.tile([P, J // 16], U16, name="offsets")
         half_list = [offsets[:, h * HALF // 16 : (h + 1) * HALF // 16] for h in range(2)]
@@ -64,39 +64,53 @@ def tile_list_xcross_mix_relu_kernel(
         tab_w = [held(f"tab_w{a}", [P, T], I32) for a in range(2)]
         dn_raw0 = held("dn_raw0", [P, R], I32)
         dn_raw1 = [held(f"dn_raw1_{c}", [P, K_PASS], I32) for c in range(2)]
+        dn_raw = [[dn_raw0[:, 0:K_PASS], dn_raw0[:, K_PASS:R]], [dn_raw1[0][:], dn_raw1[1][:]]]
         x0 = [held(f"x0_{c}", [P, T], F32) for c in range(2)]
         wb8_w = held("wb8_w", [P, N], I32)
         wb4_w = held("wb4_w", [P, 2 * N], U8)
         bias = held("bias", [P, 2], F32)
         up_raw = [held(f"up_raw{c}", [P, PACK, N], F32) for c in range(2)]
 
-        nc.sync.dma_start(offsets[:], offs)
-        for quad in range(QUADS):
-            load_scale_rows(nc.scalar, tab_plane, tab_scales, quad)
-        for quad in range(QUADS):
-            load_scale_rows(nc.scalar, dn_plane_raw, dn_scales, quad)
-        with nc.allow_non_contiguous_dma(reason="one bias value a partition"):
-            nc.gpsimd.dma_start(out=bias[:], in_=b.rearrange("(c p) -> p c", p=P))
-        nc.sync.dma_start(out=tab_w[0][:], in_=words_of(tab_words, 0))
-        nc.sync.dma_start(out=dn_raw0[:], in_=words_of(dn_words, 0))
-        nc.sync.dma_start(out=tab_w[1][:], in_=words_of(tab_words, 1))
-        for c in range(2):
-            nc.sync.dma_start(out=dn_raw1[c][:], in_=words_of(dn_words, 1)[:, c * K_PASS : (c + 1) * K_PASS])
-        for c, (plane, scales) in enumerate(((wb8_plane, wb8_scales), (wb4_plane, wb4_scales))):
-            nc.sync.dma_start(out=x0[c][:], in_=x0T[c * P : (c + 1) * P, :])
-            for quad in range(QUADS):
-                load_scale_rows(nc.scalar, plane, scales, quad)
-        nc.sync.dma_start(out=wb8_w[:], in_=words_of(wb8_words, 0))
-        nc.sync.dma_start(out=wb4_w[:].bitcast(I32), in_=wb4_words[0].bitcast(I32))
-        for c in range(2):
+        def load_dn(a, c):
+            nc.sync.dma_start(out=dn_raw[a][c], in_=words_of(dn_words, a)[:, c * K_PASS : (c + 1) * K_PASS])
+
+        def load_up(c):
             rows = upw[c * K_PASS : (c + 1) * K_PASS, :].rearrange("(g t q) n -> t g q n", t=PACK, q=8)
             for t in range(PACK):
                 nc.sync.dma_start(out=up_raw[c][:, t, :], in_=rows[t])
 
+        with nc.allow_non_contiguous_dma(reason="one bias value a partition"):
+            nc.gpsimd.dma_start(out=bias[:], in_=b.rearrange("(c p) -> p c", p=P))
+        for quad in range(QUADS):
+            load_scale_rows(nc.gpsimd, wb8_plane, wb8_scales, quad)
+
+        nc.sync.dma_start(offsets[:], offs)
+        nc.sync.dma_start(out=tab_w[0][:], in_=words_of(tab_words, 0))
+        for quad in range(QUADS):
+            load_scale_rows(nc.sync, tab_plane, tab_scales, quad)
+        nc.sync.dma_start(out=dn_raw0[:], in_=words_of(dn_words, 0))
+        for quad in range(QUADS):
+            load_scale_rows(nc.sync, dn_plane_raw, dn_scales, quad)
+        nc.sync.dma_start(out=tab_w[1][:], in_=words_of(tab_words, 1))
+        load_dn(1, 0)
+        for quad in (0, 1):
+            load_scale_rows(nc.sync, wb4_plane, wb4_scales, quad)
+        load_dn(1, 1)
+        nc.sync.dma_start(out=x0[0][:], in_=x0T[0:P, :])
+        for quad in (2, 3):
+            load_scale_rows(nc.sync, wb4_plane, wb4_scales, quad)
+        load_up(0)
+        nc.sync.dma_start(out=wb8_w[:], in_=words_of(wb8_words, 0))
+        nc.sync.dma_start(out=wb4_w[:].bitcast(I32), in_=wb4_words[0].bitcast(I32))
+        load_up(1)
+        nc.sync.dma_start(out=x0[1][:], in_=x0T[P : 2 * P, :])
+
         v_plane = held("v_plane", [P, J], U8)
-        v_w = [[held(f"v_w{a}_{h}", [P, HALF], U32) for h in range(2)] for a in range(2)]
+        v_tags = {(0, 1): "dn_plane_raw", (1, 1): "dn_raw1_0"}
+        v_w = [[held(f"v_w{a}_{h}", [P, HALF], U32, tag=v_tags.get((a, h))) for h in range(2)] for a in range(2)]
         dn_plane = held("dn_plane", [P, R], U8)
-        dn_w = [[held(f"dn_w{a}_{c}", [P, K_PASS], I32) for c in range(2)] for a in range(2)]
+        dn_tags = {(0, 1): "tab_w1"}
+        dn_w = [[held(f"dn_w{a}_{c}", [P, K_PASS], I32, tag=dn_tags.get((a, c))) for c in range(2)] for a in range(2)]
 
         def gather_plane(h):
             nc.vector.tensor_copy(v_plane[:, h * HALF : (h + 1) * HALF], tab_plane[:].indirect(half_list[h]))
@@ -104,35 +118,38 @@ def tile_list_xcross_mix_relu_kernel(
         def gather_words(a, h):
             nc.vector.tensor_copy(v_w[a][h][:], tab_w[a][:].bitcast(U32).indirect(half_list[h]))
 
-        def order_words(a, c, raw):
+        def order_words(a, c):
             nc.vector.tensor_copy(
                 out=dn_w[a][c][:].rearrange("p (t g q) -> p t g q", t=PACK, q=8),
-                in_=raw.rearrange("p (g t q) -> p t g q", t=PACK, q=8),
+                in_=dn_raw[a][c].rearrange("p (g t q) -> p t g q", t=PACK, q=8),
             )
 
+        x0_g = [[held(f"x0_g{m}_{h}", [P, HALF], F32) for h in range(2)] for m in range(2)]
+
+        def gather_x0(m, h):
+            nc.vector.tensor_copy(x0_g[m][h][:], x0[m][:].indirect(half_list[h]))
+
+        gather_words(0, 0)
         gather_plane(0)
         gather_plane(1)
-        gather_words(0, 0)
+        order_words(0, 0)
         nc.vector.tensor_copy(
             out=dn_plane[:].bitcast(I32).rearrange("p (c t g w) -> p c t g w", c=2, t=PACK, w=2),
             in_=dn_plane_raw[:].bitcast(I32).rearrange("p (c g t w) -> p c t g w", c=2, t=PACK, w=2),
         )
-        order_words(0, 0, dn_raw0[:, 0:K_PASS])
-        order_words(0, 1, dn_raw0[:, K_PASS:R])
-        gather_words(1, 0)
-        order_words(1, 0, dn_raw1[0][:])
-        order_words(1, 1, dn_raw1[1][:])
         gather_words(0, 1)
+        gather_words(1, 0)
+        order_words(1, 0)
         gather_words(1, 1)
+        order_words(0, 1)
+        order_words(1, 1)
+        gather_x0(0, 0)
+        gather_x0(0, 1)
 
         nc.gpsimd.dma_start(out=low_plane[0:112, :].bitcast(I32), in_=v_plane[4:116, :].bitcast(I32))
 
         bias1 = held("bias1", [P, 2], F32)
         nc.scalar.activation(bias1[:], bias[:], ACT.Copy, bias=1.0)
-
-        x0_g = [held(f"x0_g{c}", [P, J], F32) for c in range(2)]
-        for c in range(2):
-            nc.vector.tensor_copy(x0_g[c][:], x0[c][:].indirect(offsets[:]))
 
         def hs_passes(bank, a, c, h, s):
             cols = slice(s * QUARTER, (s + 1) * QUARTER)
@@ -148,65 +165,67 @@ def tile_list_xcross_mix_relu_kernel(
                     stop=(a == 1 and t == PACK - 1),
                 )
 
-        h_w = {}
-        h_plane = {}
-        for h in range(2):
-            banks = {(c, s): psum_h.tile([P, PACK, QUARTER], F32, name="hs") for c in range(2) for s in range(2)}
-            if h == 0:
-                for (c, s), bank in banks.items():
-                    hs_passes(bank, 0, c, h, s)
-            for c in range(2):
-                h_bf = held(f"h_bf{h}_{c}", [P, HALF, PACK], BF16)
+        h_bf = {}
+        for c in range(2):
+            banks = {(h, s): psum_h.tile([P, PACK, QUARTER], F32, name="hs") for h in range(2) for s in range(2)}
+            for (h, s), bank in banks.items():
+                hs_passes(bank, 0, c, h, s)
+            for h in range(2):
+                h_bf[c, h] = held(f"h_bf{c}_{h}", [P, HALF, PACK], BF16)
                 for s in range(2):
-                    if h == 1:
-                        hs_passes(banks[c, s], 0, c, h, s)
-                    hs_passes(banks[c, s], 1, c, h, s)
+                    hs_passes(banks[h, s], 1, c, h, s)
                     nc.scalar.activation(
-                        h_bf[:, s * QUARTER : (s + 1) * QUARTER, :],
-                        banks[c, s][:].rearrange("p t j -> p j t"),
+                        h_bf[c, h][:, s * QUARTER : (s + 1) * QUARTER, :],
+                        banks[h, s][:].rearrange("p t j -> p j t"),
                         ACT.Relu,
                     )
-                h_w[h, c] = held(f"h_w{h}_{c}", [P, HALF], U32)
-                h_plane[h, c] = held(f"h_plane{h}_{c}", [P, HALF], U8)
-                nc.vector.quantize_mx(
-                    out=h_w[h, c][:].bitcast(FP8X4),
-                    scales=h_plane[h, c][:],
-                    in_=h_bf[:].rearrange("p j t -> p (j t)"),
-                )
 
-        up_w = []
-        up_plane = []
-        for c in range(2):
+        h_w = {}
+        h_plane = {}
+
+        def quantize_h(c, h, codes):
+            h_w[c, h] = codes
+            h_plane[c, h] = held(f"h_plane{c}_{h}", [P, HALF], U8)
+            nc.vector.quantize_mx(
+                out=codes.bitcast(FP8X4), scales=h_plane[c, h][:], in_=h_bf[c, h][:].rearrange("p j t -> p (j t)")
+            )
+
+        up_w = {}
+        up_plane = {}
+
+        def quantize_up(c):
             up_bf = held(f"up_bf{c}", [P, N, PACK], BF16)
-            dst = up_bf[:].rearrange("p (n i) t -> p n t i", i=4)
-            src = up_raw[c][:].rearrange("p t (n i) -> p n t i", i=4)
-            if c == 0:
-                nc.scalar.copy(dst, src)
-            else:
-                nc.vector.tensor_copy(dst, src)
-            up_w.append(held(f"up_w{c}", [P, N], U32))
-            up_plane.append(held(f"up_plane{c}", [P, N], U8))
+            nc.vector.tensor_copy(up_bf[:], up_raw[c][:].rearrange("p t n -> p n t"))
+            up_w[c] = held(f"up_w{c}", [P, N], U32)
+            up_plane[c] = held(f"up_plane{c}", [P, N], U8)
             nc.vector.quantize_mx(
                 out=up_w[c][:].bitcast(FP8X4), scales=up_plane[c][:], in_=up_bf[:].rearrange("p n t -> p (n t)")
             )
 
+        quantize_h(0, 0, held("h_w0_0", [P, HALF], U32, tag="x0_0")[:])
+        quantize_up(0)
+        quantize_h(0, 1, held("h_w0_1", [P, HALF], U32, tag="up_bf0")[:])
+        quantize_up(1)
+        h_w1 = held("h_w1", [P, J], U32, tag="up_bf1")
+        quantize_h(1, 0, h_w1[:, 0:HALF])
+        quantize_h(1, 1, h_w1[:, HALF:J])
+
+        y = [psum_y.tile([P, 2, HALF], F32, name=f"y{h}") for h in range(2)]
         for h in range(2):
-            y = psum_y.tile([P, 2, HALF], F32, name=f"y{h}")
-            jcols = slice(h * HALF, (h + 1) * HALF)
             for m in range(2):
                 nc.tensor.matmul_mx(
-                    out=y[:, m, :],
+                    out=y[h][:, m, :],
                     lhsT=wb8_w[:, m * P : (m + 1) * P].bitcast(FP8X4),
                     lhsT_scale=wb8_plane[:, m * P : (m + 1) * P],
                     rhs=v_w[0][h][:].bitcast(FP8X4),
-                    rhs_scale=v_plane[:, jcols],
+                    rhs_scale=v_plane[:, h * HALF : (h + 1) * HALF],
                     start=(m == 0),
                     stop=False,
                 )
             for m in range(2):
                 for s in range(2):
                     nc.tensor.matmul_mx(
-                        out=y[:, m, s * QUARTER : (s + 1) * QUARTER],
+                        out=y[h][:, m, s * QUARTER : (s + 1) * QUARTER],
                         lhsT=wb4_w[:, 2 * m * P : 2 * (m + 1) * P].bitcast(FP4X4),
                         lhsT_scale=wb4_plane[:, m * P : (m + 1) * P],
                         rhs=v_w[1][h][:, s * QUARTER : (s + 1) * QUARTER].bitcast(FP8X4),
@@ -214,20 +233,23 @@ def tile_list_xcross_mix_relu_kernel(
                         start=False,
                         stop=False,
                     )
-            for c in range(2):
+        for c in range(2):
+            for h in range(2):
                 for m in range(2):
                     nc.tensor.matmul_mx(
-                        out=y[:, m, :],
+                        out=y[h][:, m, :],
                         lhsT=up_w[c][:, m * P : (m + 1) * P].bitcast(FP8X4),
                         lhsT_scale=up_plane[c][:, m * P : (m + 1) * P],
-                        rhs=h_w[h, c][:].bitcast(FP8X4),
-                        rhs_scale=h_plane[h, c][:],
+                        rhs=h_w[c, h].bitcast(FP8X4),
+                        rhs_scale=h_plane[c, h][:],
                         start=False,
                         stop=(c == 1 and m == 1),
                     )
+        for h in range(2):
+            gather_x0(1, h)
             for m in range(2):
                 res = held(f"res{h}_{m}", [P, HALF], F32)
                 nc.vector.scalar_tensor_tensor(
-                    out=res[:], in0=y[:, m, :], scalar=bias1[:, m : m + 1], in1=x0_g[m][:, jcols], op0=ALU.add, op1=ALU.mult
+                    out=res[:], in0=y[h][:, m, :], scalar=bias1[:, m : m + 1], in1=x0_g[m][h][:], op0=ALU.add, op1=ALU.mult
                 )
-                nc.sync.dma_start(out=out[m * P : (m + 1) * P, jcols], in_=res[:])
+                nc.sync.dma_start(out=out[m * P : (m + 1) * P, h * HALF : (h + 1) * HALF], in_=res[:])

@@ -31,7 +31,7 @@ def tile_list_xcross_mix_relu_kernel(
     with ExitStack() as ctx:
         lists = ctx.enter_context(tc.tile_pool(name="lists", bufs=1))
         keep = ctx.enter_context(tc.tile_pool(name="keep", bufs=1))
-        psum_h = ctx.enter_context(tc.psum_pool(name="psum_h", bufs=6))
+        psum_h = ctx.enter_context(tc.psum_pool(name="psum_h", bufs=4))
         psum_y = ctx.enter_context(tc.psum_pool(name="psum_y", bufs=1))
 
         def held(name, shape, dtype, tag=None):
@@ -44,12 +44,10 @@ def tile_list_xcross_mix_relu_kernel(
         dn_plane_raw = held("dn_plane_raw", [P, R], U8)
         wb8_plane = held("wb8_plane", [P, N], U8)
         wb4_plane = held("wb4_plane", [P, N], U8)
-        low_plane = held("low_plane", [P, J], U8)
         nc.vector.memset(tab_plane[:].bitcast(I32), 0)
         nc.vector.memset(dn_plane_raw[:].bitcast(I32), 0)
-        nc.vector.memset(wb8_plane[:].bitcast(I32), 0)
+        nc.gpsimd.memset(wb8_plane[:].bitcast(I32), 0)
         nc.vector.memset(wb4_plane[:].bitcast(I32), 0)
-        nc.vector.memset(low_plane[:].bitcast(I32), 0)
 
         def load_scale_rows(queue, plane, scales, quad):
             passes = scales.shape[0]
@@ -68,7 +66,6 @@ def tile_list_xcross_mix_relu_kernel(
         x0 = [held(f"x0_{c}", [P, T], F32) for c in range(2)]
         wb8_w = held("wb8_w", [P, N], I32)
         wb4_w = held("wb4_w", [P, 2 * N], U8)
-        bias = held("bias", [P, 2], F32)
         up_raw = [held(f"up_raw{c}", [P, PACK, N], F32) for c in range(2)]
 
         def load_dn(a, c):
@@ -79,6 +76,7 @@ def tile_list_xcross_mix_relu_kernel(
             for t in range(PACK):
                 nc.sync.dma_start(out=up_raw[c][:, t, :], in_=rows[t])
 
+        bias = held("bias", [P, 2], F32)
         with nc.allow_non_contiguous_dma(reason="one bias value a partition"):
             nc.gpsimd.dma_start(out=bias[:], in_=b.rearrange("(c p) -> p c", p=P))
         for quad in range(QUADS):
@@ -112,9 +110,6 @@ def tile_list_xcross_mix_relu_kernel(
         dn_tags = {(0, 1): "tab_w1"}
         dn_w = [[held(f"dn_w{a}_{c}", [P, K_PASS], I32, tag=dn_tags.get((a, c))) for c in range(2)] for a in range(2)]
 
-        def gather_plane(h):
-            nc.vector.tensor_copy(v_plane[:, h * HALF : (h + 1) * HALF], tab_plane[:].indirect(half_list[h]))
-
         def gather_words(a, h):
             nc.vector.tensor_copy(v_w[a][h][:], tab_w[a][:].bitcast(U32).indirect(half_list[h]))
 
@@ -124,14 +119,10 @@ def tile_list_xcross_mix_relu_kernel(
                 in_=dn_raw[a][c].rearrange("p (g t q) -> p t g q", t=PACK, q=8),
             )
 
-        x0_g = [[held(f"x0_g{m}_{h}", [P, HALF], F32) for h in range(2)] for m in range(2)]
-
-        def gather_x0(m, h):
-            nc.vector.tensor_copy(x0_g[m][h][:], x0[m][:].indirect(half_list[h]))
+        x0_g = held("x0_g", [P, J], F32)
 
         gather_words(0, 0)
-        gather_plane(0)
-        gather_plane(1)
+        nc.vector.tensor_copy(v_plane[:], tab_plane[:].indirect(offsets[:]))
         order_words(0, 0)
         nc.vector.tensor_copy(
             out=dn_plane[:].bitcast(I32).rearrange("p (c t g w) -> p c t g w", c=2, t=PACK, w=2),
@@ -143,11 +134,11 @@ def tile_list_xcross_mix_relu_kernel(
         gather_words(1, 1)
         order_words(0, 1)
         order_words(1, 1)
-        gather_x0(0, 0)
-        gather_x0(0, 1)
+        nc.vector.tensor_copy(x0_g[:], x0[0][:].indirect(offsets[:]))
 
+        low_plane = held("low_plane", [P, J], U8, tag="tab_w0")
+        nc.gpsimd.memset(low_plane[:].bitcast(I32), 0)
         nc.gpsimd.dma_start(out=low_plane[0:112, :].bitcast(I32), in_=v_plane[4:116, :].bitcast(I32))
-
         bias1 = held("bias1", [P, 2], F32)
         nc.scalar.activation(bias1[:], bias[:], ACT.Copy, bias=1.0)
 
@@ -190,42 +181,35 @@ def tile_list_xcross_mix_relu_kernel(
                 out=codes.bitcast(FP8X4), scales=h_plane[c, h][:], in_=h_bf[c, h][:].rearrange("p j t -> p (j t)")
             )
 
-        up_w = {}
-        up_plane = {}
-
-        def quantize_up(c):
-            up_bf = held(f"up_bf{c}", [P, N, PACK], BF16)
-            nc.vector.tensor_copy(up_bf[:], up_raw[c][:].rearrange("p t n -> p n t"))
-            up_w[c] = held(f"up_w{c}", [P, N], U32)
-            up_plane[c] = held(f"up_plane{c}", [P, N], U8)
+        up_bf = [held(f"up_bf{c}", [P, N, PACK], BF16) for c in range(2)]
+        up_w = [held(f"up_w{c}", [P, N], U32) for c in range(2)]
+        up_plane = [held(f"up_plane{c}", [P, N], U8) for c in range(2)]
+        for c in range(2):
+            nc.vector.tensor_copy(up_bf[c][:], up_raw[c][:].rearrange("p t n -> p n t"))
+            quantize_h(0, c, held(f"h_w0_{c}", [P, HALF], U32, tag=f"up_raw{c}")[:])
             nc.vector.quantize_mx(
-                out=up_w[c][:].bitcast(FP8X4), scales=up_plane[c][:], in_=up_bf[:].rearrange("p n t -> p (n t)")
+                out=up_w[c][:].bitcast(FP8X4), scales=up_plane[c][:], in_=up_bf[c][:].rearrange("p n t -> p (n t)")
             )
-
-        quantize_h(0, 0, held("h_w0_0", [P, HALF], U32, tag="x0_0")[:])
-        quantize_up(0)
-        quantize_h(0, 1, held("h_w0_1", [P, HALF], U32, tag="up_bf0")[:])
-        quantize_up(1)
         h_w1 = held("h_w1", [P, J], U32, tag="up_bf1")
         quantize_h(1, 0, h_w1[:, 0:HALF])
         quantize_h(1, 1, h_w1[:, HALF:J])
 
-        y = [psum_y.tile([P, 2, HALF], F32, name=f"y{h}") for h in range(2)]
+        y = [[psum_y.tile([P, HALF], F32, name=f"y{h}_{m}") for m in range(2)] for h in range(2)]
         for h in range(2):
             for m in range(2):
                 nc.tensor.matmul_mx(
-                    out=y[h][:, m, :],
+                    out=y[h][m][:],
                     lhsT=wb8_w[:, m * P : (m + 1) * P].bitcast(FP8X4),
                     lhsT_scale=wb8_plane[:, m * P : (m + 1) * P],
                     rhs=v_w[0][h][:].bitcast(FP8X4),
                     rhs_scale=v_plane[:, h * HALF : (h + 1) * HALF],
-                    start=(m == 0),
+                    start=True,
                     stop=False,
                 )
             for m in range(2):
                 for s in range(2):
                     nc.tensor.matmul_mx(
-                        out=y[h][:, m, s * QUARTER : (s + 1) * QUARTER],
+                        out=y[h][m][:, s * QUARTER : (s + 1) * QUARTER],
                         lhsT=wb4_w[:, 2 * m * P : 2 * (m + 1) * P].bitcast(FP4X4),
                         lhsT_scale=wb4_plane[:, m * P : (m + 1) * P],
                         rhs=v_w[1][h][:, s * QUARTER : (s + 1) * QUARTER].bitcast(FP8X4),
@@ -235,21 +219,24 @@ def tile_list_xcross_mix_relu_kernel(
                     )
         for c in range(2):
             for h in range(2):
-                for m in range(2):
+                for m in (1, 0):
                     nc.tensor.matmul_mx(
-                        out=y[h][:, m, :],
+                        out=y[h][m][:],
                         lhsT=up_w[c][:, m * P : (m + 1) * P].bitcast(FP8X4),
                         lhsT_scale=up_plane[c][:, m * P : (m + 1) * P],
                         rhs=h_w[c, h].bitcast(FP8X4),
                         rhs_scale=h_plane[c, h][:],
                         start=False,
-                        stop=(c == 1 and m == 1),
+                        stop=(c == 1),
                     )
         for h in range(2):
-            gather_x0(1, h)
+            jcols = slice(h * HALF, (h + 1) * HALF)
+            shifted = held(f"shifted{h}", [P, HALF], F32)
+            nc.scalar.activation(shifted[:], y[h][1][:], ACT.Identity, bias=bias1[:, 1:2])
+            res = [held(f"res{m}_{h}", [P, HALF], F32) for m in range(2)]
+            nc.vector.scalar_tensor_tensor(
+                out=res[0][:], in0=y[h][0][:], scalar=bias1[:, 0:1], in1=x0_g[:, jcols], op0=ALU.add, op1=ALU.mult
+            )
+            nc.vector.tensor_tensor(res[1][:], x0[1][:].indirect(half_list[h]), shifted[:], ALU.mult)
             for m in range(2):
-                res = held(f"res{h}_{m}", [P, HALF], F32)
-                nc.vector.scalar_tensor_tensor(
-                    out=res[:], in0=y[h][:, m, :], scalar=bias1[:, m : m + 1], in1=x0_g[m][h][:], op0=ALU.add, op1=ALU.mult
-                )
-                nc.sync.dma_start(out=out[m * P : (m + 1) * P, h * HALF : (h + 1) * HALF], in_=res[:])
+                nc.sync.dma_start(out=out[m * P : (m + 1) * P, jcols], in_=res[m][:])

@@ -18,10 +18,15 @@ ALU = mybir.AluOpType
 
 P = 128
 PACK = 4
-K_PASS = P * PACK
+PASS = P * PACK
+GROUP = 8
+QUADRANT = 32
+QUADS = P // QUADRANT
+ROWS = QUADRANT // GROUP
+PER_COLUMN = 16
 HALF = J // 2
 QUARTER = J // 4
-QUADS = 4
+SHIFT_ROWS = 112
 
 
 def tile_list_xcross_mix_relu_kernel(
@@ -34,92 +39,77 @@ def tile_list_xcross_mix_relu_kernel(
         psum_h = ctx.enter_context(tc.psum_pool(name="psum_h", bufs=4))
         psum_y = ctx.enter_context(tc.psum_pool(name="psum_y", bufs=1))
 
-        def held(name, shape, dtype, tag=None):
-            return keep.tile(shape, dtype, name=name, tag=tag or name, align_bytes=64)
+        def held(name, shape, dtype, after=None):
+            return keep.tile(shape, dtype, name=name, tag=after or name, align_bytes=64)
 
-        offsets = lists.tile([P, J // 16], U16, name="offsets")
-        half_list = [offsets[:, h * HALF // 16 : (h + 1) * HALF // 16] for h in range(2)]
+        offsets = lists.tile([P, J // PER_COLUMN], U16, name="offsets")
+        half_list = [offsets[:, h * HALF // PER_COLUMN : (h + 1) * HALF // PER_COLUMN] for h in range(2)]
 
         tab_plane = held("tab_plane", [P, T], U8)
         dn_plane_raw = held("dn_plane_raw", [P, R], U8)
         wb8_plane = held("wb8_plane", [P, N], U8)
         wb4_plane = held("wb4_plane", [P, N], U8)
-        nc.vector.memset(tab_plane[:].bitcast(I32), 0)
-        nc.vector.memset(dn_plane_raw[:].bitcast(I32), 0)
-        nc.gpsimd.memset(wb8_plane[:].bitcast(I32), 0)
-        nc.vector.memset(wb4_plane[:].bitcast(I32), 0)
+        for plane in (tab_plane, dn_plane_raw, wb8_plane, wb4_plane):
+            nc.vector.memset(plane[:].bitcast(I32), 0)
 
-        def load_scale_rows(queue, plane, scales, quad):
+        def load_scale_rows(plane, scales, quads):
             passes = scales.shape[0]
-            queue.dma_start(
-                out=plane[32 * quad : 32 * quad + 4 * passes, :].bitcast(I32),
-                in_=scales[:, 4 * quad : 4 * quad + 4, :].bitcast(I32),
-            )
+            for quad in quads:
+                nc.sync.dma_start(
+                    out=plane[QUADRANT * quad : QUADRANT * quad + ROWS * passes, :].bitcast(I32),
+                    in_=scales[:, ROWS * quad : ROWS * (quad + 1), :].bitcast(I32),
+                )
 
         def words_of(words, a):
             return words[a].rearrange("p c i -> p (c i)").bitcast(I32)
 
         tab_w = [held(f"tab_w{a}", [P, T], I32) for a in range(2)]
         dn_raw0 = held("dn_raw0", [P, R], I32)
-        dn_raw1 = [held(f"dn_raw1_{c}", [P, K_PASS], I32) for c in range(2)]
-        dn_raw = [[dn_raw0[:, 0:K_PASS], dn_raw0[:, K_PASS:R]], [dn_raw1[0][:], dn_raw1[1][:]]]
-        x0 = [held(f"x0_{c}", [P, T], F32) for c in range(2)]
+        dn_raw1 = [held(f"dn_raw1_{c}", [P, PASS], I32) for c in range(2)]
+        dn_raw = [[dn_raw0[:, 0:PASS], dn_raw0[:, PASS:R]], [dn_raw1[0][:], dn_raw1[1][:]]]
+        x0 = [held(f"x0_{m}", [P, T], F32) for m in range(2)]
         wb8_w = held("wb8_w", [P, N], I32)
         wb4_w = held("wb4_w", [P, 2 * N], U8)
         up_raw = [held(f"up_raw{c}", [P, PACK, N], F32) for c in range(2)]
 
-        def load_dn(a, c):
-            nc.sync.dma_start(out=dn_raw[a][c], in_=words_of(dn_words, a)[:, c * K_PASS : (c + 1) * K_PASS])
-
-        def load_up(c):
-            rows = upw[c * K_PASS : (c + 1) * K_PASS, :].rearrange("(g t q) n -> t g q n", t=PACK, q=8)
-            for t in range(PACK):
-                nc.sync.dma_start(out=up_raw[c][:, t, :], in_=rows[t])
-
         bias = held("bias", [P, 2], F32)
         with nc.allow_non_contiguous_dma(reason="one bias value a partition"):
-            nc.gpsimd.dma_start(out=bias[:], in_=b.rearrange("(c p) -> p c", p=P))
-        for quad in range(QUADS):
-            load_scale_rows(nc.gpsimd, wb8_plane, wb8_scales, quad)
+            nc.gpsimd.dma_start(out=bias[:], in_=b.rearrange("(m p) -> p m", p=P))
 
         nc.sync.dma_start(offsets[:], offs)
         nc.sync.dma_start(out=tab_w[0][:], in_=words_of(tab_words, 0))
-        for quad in range(QUADS):
-            load_scale_rows(nc.sync, tab_plane, tab_scales, quad)
+        load_scale_rows(tab_plane, tab_scales, range(QUADS))
         nc.sync.dma_start(out=dn_raw0[:], in_=words_of(dn_words, 0))
-        for quad in range(QUADS):
-            load_scale_rows(nc.sync, dn_plane_raw, dn_scales, quad)
+        load_scale_rows(dn_plane_raw, dn_scales, range(QUADS))
         nc.sync.dma_start(out=tab_w[1][:], in_=words_of(tab_words, 1))
-        load_dn(1, 0)
-        for quad in (0, 1):
-            load_scale_rows(nc.sync, wb4_plane, wb4_scales, quad)
-        load_dn(1, 1)
+        nc.sync.dma_start(out=dn_raw[1][0], in_=words_of(dn_words, 1)[:, 0:PASS])
+        load_scale_rows(wb4_plane, wb4_scales, range(0, QUADS // 2))
+        nc.sync.dma_start(out=dn_raw[1][1], in_=words_of(dn_words, 1)[:, PASS:R])
         nc.sync.dma_start(out=x0[0][:], in_=x0T[0:P, :])
-        for quad in (2, 3):
-            load_scale_rows(nc.sync, wb4_plane, wb4_scales, quad)
-        load_up(0)
+        load_scale_rows(wb4_plane, wb4_scales, range(QUADS // 2, QUADS))
+        for c in range(2):
+            rows = upw[c * PASS : (c + 1) * PASS, :].rearrange("(g t q) n -> t g q n", t=PACK, q=GROUP)
+            for t in range(PACK):
+                nc.sync.dma_start(out=up_raw[c][:, t, :], in_=rows[t])
         nc.sync.dma_start(out=wb8_w[:], in_=words_of(wb8_words, 0))
         nc.sync.dma_start(out=wb4_w[:].bitcast(I32), in_=wb4_words[0].bitcast(I32))
-        load_up(1)
-        nc.sync.dma_start(out=x0[1][:], in_=x0T[P : 2 * P, :])
 
         v_plane = held("v_plane", [P, J], U8)
-        v_tags = {(0, 1): "dn_plane_raw", (1, 1): "dn_raw1_0"}
-        v_w = [[held(f"v_w{a}_{h}", [P, HALF], U32, tag=v_tags.get((a, h))) for h in range(2)] for a in range(2)]
+        v_after = {(0, 1): "dn_plane_raw", (1, 1): "dn_raw1_0"}
+        v_w = [[held(f"v_w{a}_{h}", [P, HALF], U32, after=v_after.get((a, h))) for h in range(2)] for a in range(2)]
         dn_plane = held("dn_plane", [P, R], U8)
-        dn_tags = {(0, 1): "tab_w1"}
-        dn_w = [[held(f"dn_w{a}_{c}", [P, K_PASS], I32, tag=dn_tags.get((a, c))) for c in range(2)] for a in range(2)]
+        dn_after = {(0, 1): "tab_w1"}
+        dn_w = [[held(f"dn_w{a}_{c}", [P, PASS], I32, after=dn_after.get((a, c))) for c in range(2)] for a in range(2)]
+        x0_picked = held("x0_picked", [P, J], F32)
 
         def gather_words(a, h):
             nc.vector.tensor_copy(v_w[a][h][:], tab_w[a][:].bitcast(U32).indirect(half_list[h]))
 
         def order_words(a, c):
             nc.vector.tensor_copy(
-                out=dn_w[a][c][:].rearrange("p (t g q) -> p t g q", t=PACK, q=8),
-                in_=dn_raw[a][c].rearrange("p (g t q) -> p t g q", t=PACK, q=8),
+                out=dn_w[a][c][:].rearrange("p (t g q) -> p t g q", t=PACK, q=GROUP),
+                in_=dn_raw[a][c].rearrange("p (g t q) -> p t g q", t=PACK, q=GROUP),
             )
-
-        x0_g = held("x0_g", [P, J], F32)
 
         gather_words(0, 0)
         nc.vector.tensor_copy(v_plane[:], tab_plane[:].indirect(offsets[:]))
@@ -134,24 +124,28 @@ def tile_list_xcross_mix_relu_kernel(
         gather_words(1, 1)
         order_words(0, 1)
         order_words(1, 1)
-        nc.vector.tensor_copy(x0_g[:], x0[0][:].indirect(offsets[:]))
+        nc.vector.tensor_copy(x0_picked[:], x0[0][:].indirect(offsets[:]))
 
-        low_plane = held("low_plane", [P, J], U8, tag="tab_w0")
-        nc.gpsimd.memset(low_plane[:].bitcast(I32), 0)
-        nc.gpsimd.dma_start(out=low_plane[0:112, :].bitcast(I32), in_=v_plane[4:116, :].bitcast(I32))
+        v1_plane = held("v1_plane", [P, J], U8)
+        nc.vector.memset(v1_plane[:].bitcast(I32), 0)
+        nc.sync.dma_start(
+            out=v1_plane[0:SHIFT_ROWS, :].bitcast(I32), in_=v_plane[ROWS : ROWS + SHIFT_ROWS, :].bitcast(I32)
+        )
+        load_scale_rows(wb8_plane, wb8_scales, range(QUADS))
+        nc.sync.dma_start(out=x0[1][:], in_=x0T[P : 2 * P, :])
+
         bias1 = held("bias1", [P, 2], F32)
         nc.scalar.activation(bias1[:], bias[:], ACT.Copy, bias=1.0)
 
         def hs_passes(bank, a, c, h, s):
-            cols = slice(s * QUARTER, (s + 1) * QUARTER)
-            jcols = slice(h * HALF + s * QUARTER, h * HALF + (s + 1) * QUARTER)
+            j0 = h * HALF + s * QUARTER
             for t in range(PACK):
                 nc.tensor.matmul_mx(
                     out=bank[:, t, :],
                     lhsT=dn_w[a][c][:, t * P : (t + 1) * P].bitcast(FP8X4),
-                    lhsT_scale=dn_plane[4 * a :, c * K_PASS + t * P : c * K_PASS + (t + 1) * P],
-                    rhs=v_w[a][h][:, cols].bitcast(FP8X4),
-                    rhs_scale=v_plane[4 * a :, jcols],
+                    lhsT_scale=dn_plane[ROWS * a :, c * PASS + t * P : c * PASS + (t + 1) * P],
+                    rhs=v_w[a][h][:, s * QUARTER : (s + 1) * QUARTER].bitcast(FP8X4),
+                    rhs_scale=v_plane[ROWS * a :, j0 : j0 + QUARTER],
                     start=(a == 0 and t == 0),
                     stop=(a == 1 and t == PACK - 1),
                 )
@@ -186,38 +180,17 @@ def tile_list_xcross_mix_relu_kernel(
         up_plane = [held(f"up_plane{c}", [P, N], U8) for c in range(2)]
         for c in range(2):
             nc.vector.tensor_copy(up_bf[c][:], up_raw[c][:].rearrange("p t n -> p n t"))
-            quantize_h(0, c, held(f"h_w0_{c}", [P, HALF], U32, tag=f"up_raw{c}")[:])
+            quantize_h(0, c, held(f"h_w0_{c}", [P, HALF], U32, after=f"up_raw{c}")[:])
             nc.vector.quantize_mx(
                 out=up_w[c][:].bitcast(FP8X4), scales=up_plane[c][:], in_=up_bf[c][:].rearrange("p n t -> p (n t)")
             )
-        h_w1 = held("h_w1", [P, J], U32, tag="up_bf1")
-        quantize_h(1, 0, h_w1[:, 0:HALF])
-        quantize_h(1, 1, h_w1[:, HALF:J])
+        h_w1 = held("h_w1", [P, J], U32, after="up_bf1")
+        for h in range(2):
+            quantize_h(1, h, h_w1[:, h * HALF : (h + 1) * HALF])
 
         y = [[psum_y.tile([P, HALF], F32, name=f"y{h}_{m}") for m in range(2)] for h in range(2)]
-        for h in range(2):
-            for m in range(2):
-                nc.tensor.matmul_mx(
-                    out=y[h][m][:],
-                    lhsT=wb8_w[:, m * P : (m + 1) * P].bitcast(FP8X4),
-                    lhsT_scale=wb8_plane[:, m * P : (m + 1) * P],
-                    rhs=v_w[0][h][:].bitcast(FP8X4),
-                    rhs_scale=v_plane[:, h * HALF : (h + 1) * HALF],
-                    start=True,
-                    stop=False,
-                )
-            for m in range(2):
-                for s in range(2):
-                    nc.tensor.matmul_mx(
-                        out=y[h][m][:, s * QUARTER : (s + 1) * QUARTER],
-                        lhsT=wb4_w[:, 2 * m * P : 2 * (m + 1) * P].bitcast(FP4X4),
-                        lhsT_scale=wb4_plane[:, m * P : (m + 1) * P],
-                        rhs=v_w[1][h][:, s * QUARTER : (s + 1) * QUARTER].bitcast(FP8X4),
-                        rhs_scale=low_plane[:, h * HALF + s * QUARTER : h * HALF + (s + 1) * QUARTER],
-                        start=False,
-                        stop=False,
-                    )
-        for c in range(2):
+
+        def up_passes(c):
             for h in range(2):
                 for m in (1, 0):
                     nc.tensor.matmul_mx(
@@ -229,14 +202,42 @@ def tile_list_xcross_mix_relu_kernel(
                         start=False,
                         stop=(c == 1),
                     )
+
+        for h in range(2):
+            for m in range(2):
+                for s in range(2):
+                    j0 = h * HALF + s * QUARTER
+                    nc.tensor.matmul_mx(
+                        out=y[h][m][:, s * QUARTER : (s + 1) * QUARTER],
+                        lhsT=wb4_w[:, 2 * m * P : 2 * (m + 1) * P].bitcast(FP4X4),
+                        lhsT_scale=wb4_plane[:, m * P : (m + 1) * P],
+                        rhs=v_w[1][h][:, s * QUARTER : (s + 1) * QUARTER].bitcast(FP8X4),
+                        rhs_scale=v1_plane[:, j0 : j0 + QUARTER],
+                        start=(s == 0),
+                        stop=False,
+                    )
+        up_passes(0)
+        for h in range(2):
+            for m in range(2):
+                nc.tensor.matmul_mx(
+                    out=y[h][m][:],
+                    lhsT=wb8_w[:, m * P : (m + 1) * P].bitcast(FP8X4),
+                    lhsT_scale=wb8_plane[:, m * P : (m + 1) * P],
+                    rhs=v_w[0][h][:].bitcast(FP8X4),
+                    rhs_scale=v_plane[:, h * HALF : (h + 1) * HALF],
+                    start=False,
+                    stop=False,
+                )
+        up_passes(1)
+
         for h in range(2):
             jcols = slice(h * HALF, (h + 1) * HALF)
-            shifted = held(f"shifted{h}", [P, HALF], F32)
-            nc.scalar.activation(shifted[:], y[h][1][:], ACT.Identity, bias=bias1[:, 1:2])
+            biased = held(f"biased{h}", [P, HALF], F32)
+            nc.scalar.activation(biased[:], y[h][1][:], ACT.Identity, bias=bias1[:, 1:2])
             res = [held(f"res{m}_{h}", [P, HALF], F32) for m in range(2)]
             nc.vector.scalar_tensor_tensor(
-                out=res[0][:], in0=y[h][0][:], scalar=bias1[:, 0:1], in1=x0_g[:, jcols], op0=ALU.add, op1=ALU.mult
+                out=res[0][:], in0=y[h][0][:], scalar=bias1[:, 0:1], in1=x0_picked[:, jcols], op0=ALU.add, op1=ALU.mult
             )
-            nc.vector.tensor_tensor(res[1][:], x0[1][:].indirect(half_list[h]), shifted[:], ALU.mult)
+            nc.vector.tensor_tensor(res[1][:], x0[1][:].indirect(half_list[h]), biased[:], ALU.mult)
             for m in range(2):
                 nc.sync.dma_start(out=out[m * P : (m + 1) * P, jcols], in_=res[m][:])

@@ -1,3 +1,4 @@
+import math
 from contextlib import ExitStack
 
 import concourse.mybir as mybir
@@ -39,100 +40,175 @@ def tile_list_xcross_mix_relu_kernel(
         psum_h = ctx.enter_context(tc.psum_pool(name="psum_h", bufs=4))
         psum_y = ctx.enter_context(tc.psum_pool(name="psum_y", bufs=1))
 
+        place = {"end": 0}
+        width = {F32: 4, I32: 4, U32: 4, BF16: 2, U8: 1}
+
         def held(name, shape, dtype, after=None):
-            return keep.tile(shape, dtype, name=name, tag=after or name, align_bytes=64)
+            if after is None:
+                place[name] = place["end"]
+                place["end"] = place["end"] + math.prod(shape[1:]) * width[dtype] + 63 & -64
+            else:
+                place[name] = place[after[0]] + after[1]
+            return keep.tile(shape, dtype, name=name, align_bytes=64, offset=place[name])
 
         offsets = lists.tile([P, J // PER_COLUMN], U16, name="offsets")
         half_list = [offsets[:, h * HALF // PER_COLUMN : (h + 1) * HALF // PER_COLUMN] for h in range(2)]
 
         tab_plane = held("tab_plane", [P, T], U8)
         dn_plane_raw = held("dn_plane_raw", [P, R], U8)
-        wb8_plane = held("wb8_plane", [P, N], U8)
-        wb4_plane = held("wb4_plane", [P, N], U8)
-        for plane in (tab_plane, dn_plane_raw, wb8_plane, wb4_plane):
-            nc.vector.memset(plane[:].bitcast(I32), 0)
+        late_planes = held("late_planes", [P, 2 * N + J], U8)
+        wb8_plane = late_planes[:, 0:N]
+        wb4_plane = late_planes[:, N : 2 * N]
+        v1_plane = late_planes[:, 2 * N : 2 * N + J]
+        nc.vector.memset(tab_plane[:].bitcast(I32), 0)
+        nc.vector.memset(dn_plane_raw[:].bitcast(I32), 0)
+        nc.vector.memset(late_planes[:].bitcast(I32), 0)
 
-        def load_scale_rows(plane, scales, quads):
+        def scale_rows(queue, plane, scales, quad):
             passes = scales.shape[0]
-            for quad in quads:
-                nc.sync.dma_start(
-                    out=plane[QUADRANT * quad : QUADRANT * quad + ROWS * passes, :].bitcast(I32),
-                    in_=scales[:, ROWS * quad : ROWS * (quad + 1), :].bitcast(I32),
-                )
+            queue.dma_start(
+                out=plane[QUADRANT * quad : QUADRANT * quad + ROWS * passes, :].bitcast(I32),
+                in_=scales[:, ROWS * quad : ROWS * (quad + 1), :].bitcast(I32),
+            )
 
         def words_of(words, a):
             return words[a].rearrange("p c i -> p (c i)").bitcast(I32)
 
         tab_w = [held(f"tab_w{a}", [P, T], I32) for a in range(2)]
-        dn_raw0 = held("dn_raw0", [P, R], I32)
-        dn_raw1 = [held(f"dn_raw1_{c}", [P, PASS], I32) for c in range(2)]
-        dn_raw = [[dn_raw0[:, 0:PASS], dn_raw0[:, PASS:R]], [dn_raw1[0][:], dn_raw1[1][:]]]
+        dn_raw0 = [held(f"dn_raw{a}_0", [P, PASS], I32) for a in range(2)]
+        dn_raw1 = held("dn_raw_1", [P, 2, PASS], I32)
+        dn_raw = [[dn_raw0[a][:], dn_raw1[:, a, :]] for a in range(2)]
         x0 = [held(f"x0_{m}", [P, T], F32) for m in range(2)]
         wb8_w = held("wb8_w", [P, N], I32)
         wb4_w = held("wb4_w", [P, 2 * N], U8)
         up_raw = [held(f"up_raw{c}", [P, PACK, N], F32) for c in range(2)]
-
         bias = held("bias", [P, 2], F32)
-        with nc.allow_non_contiguous_dma(reason="one bias value a partition"):
-            nc.gpsimd.dma_start(out=bias[:], in_=b.rearrange("(m p) -> p m", p=P))
-
-        nc.sync.dma_start(offsets[:], offs)
-        nc.sync.dma_start(out=tab_w[0][:], in_=words_of(tab_words, 0))
-        load_scale_rows(tab_plane, tab_scales, range(QUADS))
-        nc.sync.dma_start(out=dn_raw0[:], in_=words_of(dn_words, 0))
-        load_scale_rows(dn_plane_raw, dn_scales, range(QUADS))
-        nc.sync.dma_start(out=tab_w[1][:], in_=words_of(tab_words, 1))
-        nc.sync.dma_start(out=dn_raw[1][0], in_=words_of(dn_words, 1)[:, 0:PASS])
-        load_scale_rows(wb4_plane, wb4_scales, range(0, QUADS // 2))
-        nc.sync.dma_start(out=dn_raw[1][1], in_=words_of(dn_words, 1)[:, PASS:R])
-        nc.sync.dma_start(out=x0[0][:], in_=x0T[0:P, :])
-        load_scale_rows(wb4_plane, wb4_scales, range(QUADS // 2, QUADS))
-        for c in range(2):
-            rows = upw[c * PASS : (c + 1) * PASS, :].rearrange("(g t q) n -> t g q n", t=PACK, q=GROUP)
-            for t in range(PACK):
-                nc.sync.dma_start(out=up_raw[c][:, t, :], in_=rows[t])
-        nc.sync.dma_start(out=wb8_w[:], in_=words_of(wb8_words, 0))
-        nc.sync.dma_start(out=wb4_w[:].bitcast(I32), in_=wb4_words[0].bitcast(I32))
-
         v_plane = held("v_plane", [P, J], U8)
-        v_after = {(0, 1): "dn_plane_raw", (1, 1): "dn_raw1_0"}
-        v_w = [[held(f"v_w{a}_{h}", [P, HALF], U32, after=v_after.get((a, h))) for h in range(2)] for a in range(2)]
-        dn_plane = held("dn_plane", [P, R], U8)
-        dn_after = {(0, 1): "tab_w1"}
-        dn_w = [[held(f"dn_w{a}_{c}", [P, PASS], I32, after=dn_after.get((a, c))) for c in range(2)] for a in range(2)]
-        x0_picked = held("x0_picked", [P, J], F32)
+
+        def load_up(queue, c):
+            queue.dma_start(out=up_raw[c][:], in_=upw[c * PASS : (c + 1) * PASS, :].rearrange("(p t) n -> p t n", t=PACK))
+
+        def load_bias(queue):
+            with nc.allow_non_contiguous_dma(reason="one bias value a partition"):
+                queue.dma_start(out=bias[:], in_=b.rearrange("(m p) -> p m", p=P))
+
+        def shift(queue):
+            queue.dma_start(out=v1_plane[0:SHIFT_ROWS, :].bitcast(I32), in_=v_plane[ROWS : ROWS + SHIFT_ROWS, :].bitcast(I32))
+
+        def load_tab(queue, a):
+            queue.dma_start(out=tab_w[a][:], in_=words_of(tab_words, a))
+
+        def load_dn0(queue, a):
+            queue.dma_start(out=dn_raw[a][0], in_=words_of(dn_words, a)[:, 0:PASS])
+
+        def load_dn1(queue):
+            queue.dma_start(
+                out=dn_raw1[:], in_=dn_words.rearrange("a p c i -> p a (c i)").bitcast(I32)[:, :, PASS:R]
+            )
+
+        def load_x0(queue, m):
+            queue.dma_start(out=x0[m][:], in_=x0T[m * P : (m + 1) * P, :])
+
+        def load_wb8(queue):
+            queue.dma_start(out=wb8_w[:], in_=words_of(wb8_words, 0))
+
+        def load_wb4(queue):
+            queue.dma_start(out=wb4_w[:].bitcast(I32), in_=wb4_words[0].bitcast(I32))
+
+        sync, scalar = nc.sync, nc.scalar
+        sync.dma_start(offsets[:], offs)
+        scale_rows(scalar, tab_plane, tab_scales, 0)
+        scale_rows(sync, tab_plane, tab_scales, 2)
+        scale_rows(scalar, tab_plane, tab_scales, 1)
+        scale_rows(sync, tab_plane, tab_scales, 3)
+        load_tab(sync, 0)
+        scale_rows(sync, dn_plane_raw, dn_scales, 0)
+        scale_rows(sync, dn_plane_raw, dn_scales, 1)
+        scale_rows(sync, dn_plane_raw, dn_scales, 2)
+        scale_rows(sync, dn_plane_raw, dn_scales, 3)
+        load_dn0(sync, 0)
+        load_tab(sync, 1)
+        load_dn0(sync, 1)
+        load_dn1(sync)
+        scale_rows(sync, wb8_plane, wb8_scales, 0)
+        scale_rows(sync, wb8_plane, wb8_scales, 1)
+
+        v_after = {(1, 1): ("dn_raw1_0", 0)}
+        v_w0 = held("v_w0", [P, J], U32)
+        v_w = [[v_w0[:, 0:HALF], v_w0[:, HALF:J]], [held(f"v_w1_{h}", [P, HALF], U32, after=v_after.get((1, h)))[:] for h in range(2)]]
+        dn_plane = [held(f"dn_plane{c}", [P, PASS], U8, after={}.get(c)) for c in range(2)]
+        dn_after = {}
+        dn_w1 = held("dn_w_1", [P, 2, PASS], I32, after=dn_after.get(1))
+        dn_w = [[held(f"dn_w{a}_0", [P, PASS], I32, after=dn_after.get((a, 0)))[:], dn_w1[:, a, :]] for a in range(2)]
 
         def gather_words(a, h):
-            nc.vector.tensor_copy(v_w[a][h][:], tab_w[a][:].bitcast(U32).indirect(half_list[h]))
+            nc.vector.tensor_copy(v_w[a][h], tab_w[a][:].bitcast(U32).indirect(half_list[h]))
 
         def order_words(a, c):
             nc.vector.tensor_copy(
-                out=dn_w[a][c][:].rearrange("p (t g q) -> p t g q", t=PACK, q=GROUP),
-                in_=dn_raw[a][c].rearrange("p (g t q) -> p t g q", t=PACK, q=GROUP),
+                out=dn_w[a][c].rearrange("p (t m) -> p m t", t=PACK),
+                in_=dn_raw[a][c].rearrange("p (m t) -> p m t", t=PACK),
             )
 
-        gather_words(0, 0)
-        nc.vector.tensor_copy(v_plane[:], tab_plane[:].indirect(offsets[:]))
+        def gather_first():
+            nc.vector.tensor_copy(v_w0[:], tab_w[0][:].bitcast(U32).indirect(offsets[:]))
+
+        def order_second():
+            nc.vector.tensor_copy(
+                out=dn_w1[:].rearrange("p a (t m) -> p a m t", t=PACK),
+                in_=dn_raw1[:].rearrange("p a (m t) -> p a m t", t=PACK),
+            )
+
+        def order_plane(c):
+            cols = slice(c * PASS, (c + 1) * PASS)
+            nc.vector.tensor_copy(
+                out=dn_plane[c][:].rearrange("p (t m) -> p t m", t=PACK),
+                in_=dn_plane_raw[:, cols].rearrange("p (m t) -> p t m", t=PACK),
+            )
+
+        y = [[psum_y.tile([P, HALF], F32, name=f"y{h}_{m}") for m in range(2)] for h in range(2)]
+
+        def warm(count):
+            spare = psum_h.tile([P, PACK, QUARTER], F32, name="hs")
+            for i in range(count):
+                nc.tensor.matmul_mx(
+                    out=spare[:].rearrange("p t j -> p (t j)"),
+                    lhsT=tab_w[0][:, 0:P].bitcast(FP8X4),
+                    lhsT_scale=tab_plane[:, 0:P],
+                    rhs=tab_w[0][:, 0:PASS].bitcast(FP8X4),
+                    rhs_scale=tab_plane[:, 0:PASS],
+                    start=True,
+                    stop=True,
+                )
+
+        def gather_scales():
+            nc.vector.tensor_copy(v_plane[:], tab_plane[:].indirect(offsets[:]))
+
+        gather_scales()
+        shift(sync)
+        scale_rows(sync, wb8_plane, wb8_scales, 2)
+        load_up(sync, 0)
+        scale_rows(sync, wb8_plane, wb8_scales, 3)
+        load_x0(sync, 0)
+        scale_rows(sync, wb4_plane, wb4_scales, 0)
+        load_up(sync, 1)
+        load_bias(sync)
+        scale_rows(sync, wb4_plane, wb4_scales, 1)
+        scale_rows(sync, wb4_plane, wb4_scales, 2)
+        load_x0(sync, 1)
+        load_wb8(sync)
+        load_wb4(sync)
+        scale_rows(sync, wb4_plane, wb4_scales, 3)
+        warm(2)
+        gather_first()
+        order_plane(0)
         order_words(0, 0)
-        nc.vector.tensor_copy(
-            out=dn_plane[:].bitcast(I32).rearrange("p (c t g w) -> p c t g w", c=2, t=PACK, w=2),
-            in_=dn_plane_raw[:].bitcast(I32).rearrange("p (c g t w) -> p c t g w", c=2, t=PACK, w=2),
-        )
-        gather_words(0, 1)
+        order_plane(1)
         gather_words(1, 0)
         order_words(1, 0)
         gather_words(1, 1)
-        order_words(0, 1)
-        order_words(1, 1)
-        nc.vector.tensor_copy(x0_picked[:], x0[0][:].indirect(offsets[:]))
+        order_second()
 
-        v1_plane = held("v1_plane", [P, J], U8)
-        nc.vector.memset(v1_plane[:].bitcast(I32), 0)
-        nc.sync.dma_start(
-            out=v1_plane[0:SHIFT_ROWS, :].bitcast(I32), in_=v_plane[ROWS : ROWS + SHIFT_ROWS, :].bitcast(I32)
-        )
-        load_scale_rows(wb8_plane, wb8_scales, range(QUADS))
-        nc.sync.dma_start(out=x0[1][:], in_=x0T[P : 2 * P, :])
 
         bias1 = held("bias1", [P, 2], F32)
         nc.scalar.activation(bias1[:], bias[:], ACT.Copy, bias=1.0)
@@ -143,7 +219,7 @@ def tile_list_xcross_mix_relu_kernel(
                 nc.tensor.matmul_mx(
                     out=bank[:, t, :],
                     lhsT=dn_w[a][c][:, t * P : (t + 1) * P].bitcast(FP8X4),
-                    lhsT_scale=dn_plane[ROWS * a :, c * PASS + t * P : c * PASS + (t + 1) * P],
+                    lhsT_scale=dn_plane[c][ROWS * a :, t * P : (t + 1) * P],
                     rhs=v_w[a][h][:, s * QUARTER : (s + 1) * QUARTER].bitcast(FP8X4),
                     rhs_scale=v_plane[ROWS * a :, j0 : j0 + QUARTER],
                     start=(a == 0 and t == 0),
@@ -151,93 +227,147 @@ def tile_list_xcross_mix_relu_kernel(
                 )
 
         h_bf = {}
-        for c in range(2):
-            banks = {(h, s): psum_h.tile([P, PACK, QUARTER], F32, name="hs") for h in range(2) for s in range(2)}
-            for (h, s), bank in banks.items():
-                hs_passes(bank, 0, c, h, s)
+        banks = {}
+
+        def open_banks(c):
             for h in range(2):
-                h_bf[c, h] = held(f"h_bf{c}_{h}", [P, HALF, PACK], BF16)
                 for s in range(2):
-                    hs_passes(banks[h, s], 1, c, h, s)
-                    nc.scalar.activation(
-                        h_bf[c, h][:, s * QUARTER : (s + 1) * QUARTER, :],
-                        banks[h, s][:].rearrange("p t j -> p j t"),
-                        ACT.Relu,
-                    )
+                    banks[c, h, s] = psum_h.tile([P, PACK, QUARTER], F32, name="hs")
+
+        def first_passes(c):
+            for h in range(2):
+                for s in range(2):
+                    hs_passes(banks[c, h, s], 0, c, h, s)
+
+        def relu_half(c, h, passes, after=None):
+            h_bf[c, h] = held(f"h_bf{c}_{h}", [P, HALF, PACK], BF16, after=after)
+            for s in range(2):
+                for a in passes:
+                    hs_passes(banks[c, h, s], a, c, h, s)
+                nc.scalar.activation(
+                    h_bf[c, h][:, s * QUARTER : (s + 1) * QUARTER, :],
+                    banks[c, h, s][:].rearrange("p t j -> p j t"),
+                    ACT.Relu,
+                )
 
         h_w = {}
         h_plane = {}
 
-        def quantize_h(c, h, codes):
-            h_w[c, h] = codes
+        def quantize_h(c, h, after=None):
+            h_w[c, h] = held(f"h_w{c}_{h}", [P, HALF], U32, after=after)
             h_plane[c, h] = held(f"h_plane{c}_{h}", [P, HALF], U8)
             nc.vector.quantize_mx(
-                out=codes.bitcast(FP8X4), scales=h_plane[c, h][:], in_=h_bf[c, h][:].rearrange("p j t -> p (j t)")
+                out=h_w[c, h][:].bitcast(FP8X4), scales=h_plane[c, h][:], in_=h_bf[c, h][:].rearrange("p j t -> p (j t)")
             )
 
-        up_bf = [held(f"up_bf{c}", [P, N, PACK], BF16) for c in range(2)]
-        up_w = [held(f"up_w{c}", [P, N], U32) for c in range(2)]
-        up_plane = [held(f"up_plane{c}", [P, N], U8) for c in range(2)]
-        for c in range(2):
-            nc.vector.tensor_copy(up_bf[c][:], up_raw[c][:].rearrange("p t n -> p n t"))
-            quantize_h(0, c, held(f"h_w0_{c}", [P, HALF], U32, after=f"up_raw{c}")[:])
+        up_bf = {}
+        up_w = {}
+        up_plane = {}
+
+        def round_up(c, engine="vector", after=None):
+            up_bf[c] = held(f"up_bf{c}", [P, N, PACK], BF16, after=after)
+            if engine == "vector":
+                nc.vector.tensor_copy(up_bf[c][:], up_raw[c][:].rearrange("p t n -> p n t"))
+            else:
+                nc.scalar.copy(up_bf[c][:], up_raw[c][:].rearrange("p t n -> p n t"))
+
+        def quantize_up(c, after=None):
+            up_w[c] = held(f"up_w{c}", [P, N], U32, after=after)
+            up_plane[c] = held(f"up_plane{c}", [P, N], U8)
             nc.vector.quantize_mx(
                 out=up_w[c][:].bitcast(FP8X4), scales=up_plane[c][:], in_=up_bf[c][:].rearrange("p n t -> p (n t)")
             )
-        h_w1 = held("h_w1", [P, J], U32, after="up_bf1")
-        for h in range(2):
-            quantize_h(1, h, h_w1[:, h * HALF : (h + 1) * HALF])
 
-        y = [[psum_y.tile([P, HALF], F32, name=f"y{h}_{m}") for m in range(2)] for h in range(2)]
+        picked = {}
 
-        def up_passes(c):
+        def gather_x0_whole(m, after=None):
+            both = held(f"picked{m}", [P, J], F32, after=after)
+            nc.vector.tensor_copy(both[:], x0[m][:].indirect(offsets[:]))
             for h in range(2):
-                for m in (1, 0):
+                picked[m, h] = both[:, h * HALF : (h + 1) * HALF]
+
+        def gather_x0(m, h, after=None):
+            picked[m, h] = held(f"picked{m}_{h}", [P, HALF], F32, after=after)[:]
+            nc.vector.tensor_copy(picked[m, h], x0[m][:].indirect(half_list[h]))
+
+        open_banks(0)
+        first_passes(0)
+        relu_half(0, 0, (1,))
+        relu_half(0, 1, (1,))
+        open_banks(1)
+        relu_half(1, 0, (0, 1))
+        round_up(1, "scalar")
+        relu_half(1, 1, (0, 1), after=("up_raw1", 0))
+        round_up(0)
+        quantize_h(0, 0, after=("up_raw0", 0))
+        quantize_up(0)
+        quantize_h(0, 1, after=("up_raw0", 1024))
+        gather_x0_whole(0)
+        quantize_h(1, 0, after=("x0_0", 0))
+        quantize_up(1)
+        gather_x0_whole(1)
+        quantize_h(1, 1, after=("x0_1", 0))
+
+
+        def up_passes(c, first=False, last=False, halves=(0, 1)):
+            for h in halves:
+                for m in (0, 1):
                     nc.tensor.matmul_mx(
                         out=y[h][m][:],
                         lhsT=up_w[c][:, m * P : (m + 1) * P].bitcast(FP8X4),
                         lhsT_scale=up_plane[c][:, m * P : (m + 1) * P],
-                        rhs=h_w[c, h].bitcast(FP8X4),
+                        rhs=h_w[c, h][:].bitcast(FP8X4),
                         rhs_scale=h_plane[c, h][:],
-                        start=False,
-                        stop=(c == 1),
+                        start=first,
+                        stop=last,
                     )
 
-        for h in range(2):
-            for m in range(2):
-                for s in range(2):
-                    j0 = h * HALF + s * QUARTER
+        def wb4_passes(first=False, halves=(0, 1)):
+            for h in halves:
+                for m in range(2):
+                    for s in range(2):
+                        j0 = h * HALF + s * QUARTER
+                        nc.tensor.matmul_mx(
+                            out=y[h][m][:, s * QUARTER : (s + 1) * QUARTER],
+                            lhsT=wb4_w[:, 2 * m * P : 2 * (m + 1) * P].bitcast(FP4X4),
+                            lhsT_scale=wb4_plane[:, m * P : (m + 1) * P],
+                            rhs=v_w[1][h][:, s * QUARTER : (s + 1) * QUARTER].bitcast(FP8X4),
+                            rhs_scale=v1_plane[:, j0 : j0 + QUARTER],
+                            start=(first and s == 0),
+                            stop=False,
+                        )
+
+        def wb8_passes(first=False, halves=(0, 1)):
+            for h in halves:
+                for m in range(2):
                     nc.tensor.matmul_mx(
-                        out=y[h][m][:, s * QUARTER : (s + 1) * QUARTER],
-                        lhsT=wb4_w[:, 2 * m * P : 2 * (m + 1) * P].bitcast(FP4X4),
-                        lhsT_scale=wb4_plane[:, m * P : (m + 1) * P],
-                        rhs=v_w[1][h][:, s * QUARTER : (s + 1) * QUARTER].bitcast(FP8X4),
-                        rhs_scale=v1_plane[:, j0 : j0 + QUARTER],
-                        start=(s == 0),
+                        out=y[h][m][:],
+                        lhsT=wb8_w[:, m * P : (m + 1) * P].bitcast(FP8X4),
+                        lhsT_scale=wb8_plane[:, m * P : (m + 1) * P],
+                        rhs=v_w[0][h].bitcast(FP8X4),
+                        rhs_scale=v_plane[:, h * HALF : (h + 1) * HALF],
+                        start=first,
                         stop=False,
                     )
-        up_passes(0)
-        for h in range(2):
-            for m in range(2):
-                nc.tensor.matmul_mx(
-                    out=y[h][m][:],
-                    lhsT=wb8_w[:, m * P : (m + 1) * P].bitcast(FP8X4),
-                    lhsT_scale=wb8_plane[:, m * P : (m + 1) * P],
-                    rhs=v_w[0][h][:].bitcast(FP8X4),
-                    rhs_scale=v_plane[:, h * HALF : (h + 1) * HALF],
-                    start=False,
-                    stop=False,
-                )
-        up_passes(1)
 
-        for h in range(2):
-            jcols = slice(h * HALF, (h + 1) * HALF)
-            biased = held(f"biased{h}", [P, HALF], F32)
-            nc.scalar.activation(biased[:], y[h][1][:], ACT.Identity, bias=bias1[:, 1:2])
-            res = [held(f"res{m}_{h}", [P, HALF], F32) for m in range(2)]
-            nc.vector.scalar_tensor_tensor(
-                out=res[0][:], in0=y[h][0][:], scalar=bias1[:, 0:1], in1=x0_picked[:, jcols], op0=ALU.add, op1=ALU.mult
-            )
-            nc.vector.tensor_tensor(res[1][:], x0[1][:].indirect(half_list[h]), biased[:], ALU.mult)
-            for m in range(2):
-                nc.sync.dma_start(out=out[m * P : (m + 1) * P, jcols], in_=res[m][:])
+        up_passes(0, first=True)
+        wb8_passes()
+        wb4_passes()
+        up_passes(1, last=True)
+
+        def finish(m, h, after=None, queue=nc.sync):
+            res = held(f"res{m}_{h}", [P, HALF], F32, after=after)
+            if (m, h) in picked:
+                nc.vector.scalar_tensor_tensor(
+                    out=res[:], in0=y[h][m][:], scalar=bias1[:, m : m + 1], in1=picked[m, h], op0=ALU.add, op1=ALU.mult
+                )
+            else:
+                biased = held(f"biased{m}_{h}", [P, HALF], F32)
+                nc.scalar.activation(biased[:], y[h][m][:], ACT.Identity, bias=bias1[:, m : m + 1])
+                nc.vector.tensor_tensor(res[:], x0[m][:].indirect(half_list[h]), biased[:], ALU.mult)
+            queue.dma_start(out=out[m * P : (m + 1) * P, h * HALF : (h + 1) * HALF], in_=res[:])
+
+        finish(0, 0)
+        finish(1, 0)
+        finish(0, 1)
+        finish(1, 1)

@@ -130,13 +130,13 @@ def tile_list_xcross_mix_relu_kernel(
         load_tab(sync, 1)
         load_dn0(sync, 1)
         load_dn1(sync)
-        scale_rows(sync, wb8_plane, wb8_scales, 0)
-        scale_rows(sync, wb8_plane, wb8_scales, 1)
+        scale_rows(sync, wb4_plane, wb4_scales, 0)
+        scale_rows(sync, wb4_plane, wb4_scales, 1)
 
-        v_after = {(1, 1): ("dn_raw1_0", 0)}
-        v_w0 = held("v_w0", [P, J], U32)
-        v_w = [[v_w0[:, 0:HALF], v_w0[:, HALF:J]], [held(f"v_w1_{h}", [P, HALF], U32, after=v_after.get((1, h)))[:] for h in range(2)]]
-        dn_plane = [held(f"dn_plane{c}", [P, PASS], U8, after={}.get(c)) for c in range(2)]
+        v_after = {(0, 1): ("dn_raw0_0", 0), (1, 1): ("dn_raw1_0", 0)}
+        v_w = [[held(f"v_w{a}_{h}", [P, HALF], U32, after=v_after.get((a, h)))[:] for h in range(2)] for a in range(2)]
+        dn_planes = held("dn_planes", [P, R], U8)
+        dn_plane = [dn_planes[:, c * PASS : (c + 1) * PASS] for c in range(2)]
         dn_after = {}
         dn_w1 = held("dn_w_1", [P, 2, PASS], I32, after=dn_after.get(1))
         dn_w = [[held(f"dn_w{a}_0", [P, PASS], I32, after=dn_after.get((a, 0)))[:], dn_w1[:, a, :]] for a in range(2)]
@@ -150,20 +150,16 @@ def tile_list_xcross_mix_relu_kernel(
                 in_=dn_raw[a][c].rearrange("p (m t) -> p m t", t=PACK),
             )
 
-        def gather_first():
-            nc.vector.tensor_copy(v_w0[:], tab_w[0][:].bitcast(U32).indirect(offsets[:]))
-
         def order_second():
             nc.vector.tensor_copy(
                 out=dn_w1[:].rearrange("p a (t m) -> p a m t", t=PACK),
                 in_=dn_raw1[:].rearrange("p a (m t) -> p a m t", t=PACK),
             )
 
-        def order_plane(c):
-            cols = slice(c * PASS, (c + 1) * PASS)
+        def order_planes():
             nc.vector.tensor_copy(
-                out=dn_plane[c][:].rearrange("p (t m) -> p t m", t=PACK),
-                in_=dn_plane_raw[:, cols].rearrange("p (m t) -> p t m", t=PACK),
+                out=dn_planes[:].rearrange("p (c t m) -> p c t m", c=2, t=PACK),
+                in_=dn_plane_raw[:].rearrange("p (c m t) -> p c t m", c=2, t=PACK),
             )
 
         y = [[psum_y.tile([P, HALF], F32, name=f"y{h}_{m}") for m in range(2)] for h in range(2)]
@@ -186,24 +182,24 @@ def tile_list_xcross_mix_relu_kernel(
 
         gather_scales()
         shift(sync)
-        scale_rows(sync, wb8_plane, wb8_scales, 2)
+        scale_rows(sync, wb4_plane, wb4_scales, 2)
         load_up(sync, 0)
+        scale_rows(sync, wb4_plane, wb4_scales, 3)
+        load_up(sync, 1)
+        scale_rows(sync, wb8_plane, wb8_scales, 0)
+        scale_rows(sync, wb8_plane, wb8_scales, 1)
+        scale_rows(sync, wb8_plane, wb8_scales, 2)
         scale_rows(sync, wb8_plane, wb8_scales, 3)
         load_x0(sync, 0)
-        scale_rows(sync, wb4_plane, wb4_scales, 0)
-        load_up(sync, 1)
-        load_bias(sync)
-        scale_rows(sync, wb4_plane, wb4_scales, 1)
-        scale_rows(sync, wb4_plane, wb4_scales, 2)
-        load_x0(sync, 1)
-        load_wb8(sync)
         load_wb4(sync)
-        scale_rows(sync, wb4_plane, wb4_scales, 3)
+        load_wb8(sync)
+        load_x0(sync, 1)
+        load_bias(nc.gpsimd)
         warm(2)
-        gather_first()
-        order_plane(0)
+        gather_words(0, 0)
+        order_planes()
         order_words(0, 0)
-        order_plane(1)
+        gather_words(0, 1)
         gather_words(1, 0)
         order_words(1, 0)
         gather_words(1, 1)
@@ -296,17 +292,15 @@ def tile_list_xcross_mix_relu_kernel(
         relu_half(0, 1, (1,))
         open_banks(1)
         relu_half(1, 0, (0, 1))
-        round_up(1, "scalar")
-        relu_half(1, 1, (0, 1), after=("up_raw1", 0))
+        relu_half(1, 1, (0, 1))
         round_up(0)
         quantize_h(0, 0, after=("up_raw0", 0))
         quantize_up(0)
-        quantize_h(0, 1, after=("up_raw0", 1024))
-        gather_x0_whole(0)
-        quantize_h(1, 0, after=("x0_0", 0))
+        round_up(1)
         quantize_up(1)
-        gather_x0_whole(1)
-        quantize_h(1, 1, after=("x0_1", 0))
+        quantize_h(1, 0, after=("up_raw1", 1024))
+        quantize_h(0, 1, after=("up_raw1", 0))
+        quantize_h(1, 1, after=("up_raw1", 2048))
 
 
         def up_passes(c, first=False, last=False, halves=(0, 1)):
@@ -350,10 +344,14 @@ def tile_list_xcross_mix_relu_kernel(
                         stop=False,
                     )
 
-        up_passes(0, first=True)
-        wb8_passes()
-        wb4_passes()
-        up_passes(1, last=True)
+        up_passes(0, first=True, halves=(0,))
+        wb4_passes(halves=(0,))
+        wb8_passes(halves=(0,))
+        up_passes(1, last=True, halves=(0,))
+        wb8_passes(first=True, halves=(1,))
+        wb4_passes(halves=(1,))
+        up_passes(0, halves=(1,))
+        up_passes(1, last=True, halves=(1,))
 
         def finish(m, h, after=None, queue=nc.sync):
             res = held(f"res{m}_{h}", [P, HALF], F32, after=after)
@@ -369,5 +367,5 @@ def tile_list_xcross_mix_relu_kernel(
 
         finish(0, 0)
         finish(1, 0)
-        finish(0, 1)
+        finish(0, 1, after=("biased1_0", 0))
         finish(1, 1)

@@ -190,9 +190,9 @@ def tile_list_xcross_mix_relu_kernel(
         scale_rows(sync, wb8_plane, wb8_scales, 1)
         scale_rows(sync, wb8_plane, wb8_scales, 2)
         scale_rows(sync, wb8_plane, wb8_scales, 3)
-        load_x0(sync, 0)
         load_wb4(sync)
         load_wb8(sync)
+        load_x0(sync, 0)
         load_x0(sync, 1)
         load_bias(nc.gpsimd)
         warm(2)
@@ -256,22 +256,23 @@ def tile_list_xcross_mix_relu_kernel(
                 out=h_w[c, h][:].bitcast(FP8X4), scales=h_plane[c, h][:], in_=h_bf[c, h][:].rearrange("p j t -> p (j t)")
             )
 
-        up_bf = {}
-        up_w = {}
-        up_plane = {}
+        up_bf = held("up_bf", [P, 2, N, PACK], BF16)
+        up_words = held("up_words", [P, 2, N], U32)
+        up_planes = held("up_planes", [P, 2, N], U8)
+        up_w = [up_words[:, c, :] for c in range(2)]
+        up_plane = [up_planes[:, c, :] for c in range(2)]
 
-        def round_up(c, engine="vector", after=None):
-            up_bf[c] = held(f"up_bf{c}", [P, N, PACK], BF16, after=after)
-            if engine == "vector":
-                nc.vector.tensor_copy(up_bf[c][:], up_raw[c][:].rearrange("p t n -> p n t"))
-            else:
-                nc.scalar.copy(up_bf[c][:], up_raw[c][:].rearrange("p t n -> p n t"))
+        def round_up(c):
+            nc.vector.tensor_copy(
+                up_bf[:, c, :, :].rearrange("p (n i) t -> p n t i", i=4),
+                up_raw[c][:].rearrange("p t (n i) -> p n t i", i=4),
+            )
 
-        def quantize_up(c, after=None):
-            up_w[c] = held(f"up_w{c}", [P, N], U32, after=after)
-            up_plane[c] = held(f"up_plane{c}", [P, N], U8)
+        def quantize_up():
             nc.vector.quantize_mx(
-                out=up_w[c][:].bitcast(FP8X4), scales=up_plane[c][:], in_=up_bf[c][:].rearrange("p n t -> p (n t)")
+                out=up_words[:].rearrange("p c n -> p (c n)").bitcast(FP8X4),
+                scales=up_planes[:].rearrange("p c n -> p (c n)"),
+                in_=up_bf[:].rearrange("p c n t -> p (c n t)"),
             )
 
         picked = {}
@@ -293,11 +294,10 @@ def tile_list_xcross_mix_relu_kernel(
         open_banks(1)
         relu_half(1, 0, (0, 1))
         relu_half(1, 1, (0, 1))
+        quantize_h(0, 0)
         round_up(0)
-        quantize_h(0, 0, after=("up_raw0", 0))
-        quantize_up(0)
         round_up(1)
-        quantize_up(1)
+        quantize_up()
         quantize_h(1, 0, after=("up_raw1", 1024))
         quantize_h(0, 1, after=("up_raw1", 0))
         quantize_h(1, 1, after=("up_raw1", 2048))
@@ -305,7 +305,7 @@ def tile_list_xcross_mix_relu_kernel(
 
         def up_passes(c, first=False, last=False, halves=(0, 1)):
             for h in halves:
-                for m in (0, 1):
+                for m in (h, 1 - h):
                     nc.tensor.matmul_mx(
                         out=y[h][m][:],
                         lhsT=up_w[c][:, m * P : (m + 1) * P].bitcast(FP8X4),
@@ -344,9 +344,9 @@ def tile_list_xcross_mix_relu_kernel(
                         stop=False,
                     )
 
-        up_passes(0, first=True, halves=(0,))
-        wb4_passes(halves=(0,))
+        wb4_passes(first=True, halves=(0,))
         wb8_passes(halves=(0,))
+        up_passes(0, halves=(0,))
         up_passes(1, last=True, halves=(0,))
         wb8_passes(first=True, halves=(1,))
         wb4_passes(halves=(1,))
@@ -367,5 +367,5 @@ def tile_list_xcross_mix_relu_kernel(
 
         finish(0, 0)
         finish(1, 0)
-        finish(0, 1, after=("biased1_0", 0))
         finish(1, 1)
+        finish(0, 1, after=("biased1_0", 0))

@@ -164,19 +164,6 @@ def tile_list_xcross_mix_relu_kernel(
 
         y = [[psum_y.tile([P, HALF], F32, name=f"y{h}_{m}") for m in range(2)] for h in range(2)]
 
-        def warm(count):
-            spare = psum_h.tile([P, PACK, QUARTER], F32, name="hs")
-            for i in range(count):
-                nc.tensor.matmul_mx(
-                    out=spare[:].rearrange("p t j -> p (t j)"),
-                    lhsT=tab_w[0][:, 0:P].bitcast(FP8X4),
-                    lhsT_scale=tab_plane[:, 0:P],
-                    rhs=tab_w[0][:, 0:PASS].bitcast(FP8X4),
-                    rhs_scale=tab_plane[:, 0:PASS],
-                    start=True,
-                    stop=True,
-                )
-
         def gather_scales():
             nc.vector.tensor_copy(v_plane[:], tab_plane[:].indirect(offsets[:]))
 
@@ -195,7 +182,6 @@ def tile_list_xcross_mix_relu_kernel(
         load_x0(sync, 0)
         load_x0(sync, 1)
         load_bias(nc.gpsimd)
-        warm(2)
         gather_words(0, 0)
         order_planes()
         order_words(0, 0)

@@ -83,6 +83,7 @@ def tile_list_xcross_mix_relu_kernel(
         wb4_w = held("wb4_w", [P, 2 * N], U8)
         up_raw = [held(f"up_raw{c}", [P, PACK, N], F32) for c in range(2)]
         bias = held("bias", [P, 2], F32)
+        place["end"] = place["bias"] + HALF
         v_plane = held("v_plane", [P, J], U8)
 
         def load_up(queue, c):
@@ -123,17 +124,17 @@ def tile_list_xcross_mix_relu_kernel(
         scale_rows(sync, tab_plane, tab_scales, 3)
         load_tab(sync, 0)
         scale_rows(sync, dn_plane_raw, dn_scales, 0)
+        load_dn0(sync, 0)
         scale_rows(sync, dn_plane_raw, dn_scales, 1)
         scale_rows(sync, dn_plane_raw, dn_scales, 2)
         scale_rows(sync, dn_plane_raw, dn_scales, 3)
-        load_dn0(sync, 0)
         load_tab(sync, 1)
         load_dn0(sync, 1)
         load_dn1(sync)
         scale_rows(sync, wb4_plane, wb4_scales, 0)
         scale_rows(sync, wb4_plane, wb4_scales, 1)
 
-        v_after = {(0, 1): ("dn_raw0_0", 0), (1, 1): ("dn_raw1_0", 0)}
+        v_after = {(0, 1): ("dn_plane_raw", 0), (1, 1): ("dn_raw1_0", 0)}
         v_w = [[held(f"v_w{a}_{h}", [P, HALF], U32, after=v_after.get((a, h)))[:] for h in range(2)] for a in range(2)]
         dn_planes = held("dn_planes", [P, R], U8)
         dn_plane = [dn_planes[:, c * PASS : (c + 1) * PASS] for c in range(2)]
@@ -180,11 +181,11 @@ def tile_list_xcross_mix_relu_kernel(
         load_wb4(sync)
         load_wb8(sync)
         load_x0(sync, 0)
+        load_bias(sync)
         load_x0(sync, 1)
-        load_bias(nc.gpsimd)
         gather_words(0, 0)
-        order_planes()
         order_words(0, 0)
+        order_planes()
         gather_words(0, 1)
         gather_words(1, 0)
         order_words(1, 0)
@@ -235,9 +236,9 @@ def tile_list_xcross_mix_relu_kernel(
         h_w = {}
         h_plane = {}
 
-        def quantize_h(c, h, after=None):
+        def quantize_h(c, h, after=None, plane_after=None):
             h_w[c, h] = held(f"h_w{c}_{h}", [P, HALF], U32, after=after)
-            h_plane[c, h] = held(f"h_plane{c}_{h}", [P, HALF], U8)
+            h_plane[c, h] = held(f"h_plane{c}_{h}", [P, HALF], U8, after=plane_after)
             nc.vector.quantize_mx(
                 out=h_w[c, h][:].bitcast(FP8X4), scales=h_plane[c, h][:], in_=h_bf[c, h][:].rearrange("p j t -> p (j t)")
             )
@@ -286,7 +287,8 @@ def tile_list_xcross_mix_relu_kernel(
         quantize_up()
         quantize_h(1, 0, after=("up_raw1", 1024))
         quantize_h(0, 1, after=("up_raw1", 0))
-        quantize_h(1, 1, after=("up_raw1", 2048))
+        gather_x0(0, 1)
+        quantize_h(1, 1, after=("up_raw1", 2048), plane_after=("bias", 0))
 
 
         def up_passes(c, first=False, last=False, halves=(0, 1)):

@@ -75,9 +75,7 @@ def tile_list_xcross_mix_relu_kernel(
             return words[a].rearrange("p c i -> p (c i)").bitcast(I32)
 
         tab_w = [held(f"tab_w{a}", [P, T], I32) for a in range(2)]
-        dn_raw0 = [held(f"dn_raw{a}_0", [P, PASS], I32) for a in range(2)]
-        dn_raw1 = held("dn_raw_1", [P, 2, PASS], I32)
-        dn_raw = [[dn_raw0[a][:], dn_raw1[:, a, :]] for a in range(2)]
+        dn_raw = [[held(f"dn_raw{a}_{c}", [P, PASS], I32)[:] for c in range(2)] for a in range(2)]
         x0 = [held(f"x0_{m}", [P, T], F32) for m in range(2)]
         wb8_w = held("wb8_w", [P, N], I32)
         wb4_w = held("wb4_w", [P, 2 * N], U8)
@@ -99,13 +97,8 @@ def tile_list_xcross_mix_relu_kernel(
         def load_tab(queue, a):
             queue.dma_start(out=tab_w[a][:], in_=words_of(tab_words, a))
 
-        def load_dn0(queue, a):
-            queue.dma_start(out=dn_raw[a][0], in_=words_of(dn_words, a)[:, 0:PASS])
-
-        def load_dn1(queue):
-            queue.dma_start(
-                out=dn_raw1[:], in_=dn_words.rearrange("a p c i -> p a (c i)").bitcast(I32)[:, :, PASS:R]
-            )
+        def load_dn(queue, a, c):
+            queue.dma_start(out=dn_raw[a][c], in_=words_of(dn_words, a)[:, c * PASS : (c + 1) * PASS])
 
         def load_x0(queue, m):
             queue.dma_start(out=x0[m][:], in_=x0T[m * P : (m + 1) * P, :])
@@ -116,7 +109,7 @@ def tile_list_xcross_mix_relu_kernel(
         def load_wb4(queue):
             queue.dma_start(out=wb4_w[:].bitcast(I32), in_=wb4_words[0].bitcast(I32))
 
-        sync, scalar = nc.sync, nc.scalar
+        sync, scalar, pool = nc.sync, nc.scalar, nc.gpsimd
         sync.dma_start(offsets[:], offs)
         scale_rows(scalar, tab_plane, tab_scales, 0)
         scale_rows(sync, tab_plane, tab_scales, 2)
@@ -124,43 +117,49 @@ def tile_list_xcross_mix_relu_kernel(
         scale_rows(sync, tab_plane, tab_scales, 3)
         load_tab(sync, 0)
         scale_rows(sync, dn_plane_raw, dn_scales, 0)
-        load_dn0(sync, 0)
+        load_dn(sync, 0, 0)
         scale_rows(sync, dn_plane_raw, dn_scales, 1)
         scale_rows(sync, dn_plane_raw, dn_scales, 2)
         scale_rows(sync, dn_plane_raw, dn_scales, 3)
+        load_dn(sync, 1, 0)
         load_tab(sync, 1)
-        load_dn0(sync, 1)
-        load_dn1(sync)
-        scale_rows(sync, wb4_plane, wb4_scales, 0)
-        scale_rows(sync, wb4_plane, wb4_scales, 1)
+        load_dn(sync, 0, 1)
+        load_up(sync, 0)
+        load_dn(sync, 1, 1)
+        for quad in range(QUADS):
+            scale_rows(pool, wb4_plane, wb4_scales, quad)
 
-        v_after = {(0, 1): ("dn_plane_raw", 0), (1, 1): ("dn_raw1_0", 0)}
+        v_after = {(0, 1): ("dn_plane_raw", 0)}
         v_w = [[held(f"v_w{a}_{h}", [P, HALF], U32, after=v_after.get((a, h)))[:] for h in range(2)] for a in range(2)]
-        dn_planes = held("dn_planes", [P, R], U8)
-        dn_plane = [dn_planes[:, c * PASS : (c + 1) * PASS] for c in range(2)]
-        dn_after = {}
-        dn_w1 = held("dn_w_1", [P, 2, PASS], I32, after=dn_after.get(1))
-        dn_w = [[held(f"dn_w{a}_0", [P, PASS], I32, after=dn_after.get((a, 0)))[:], dn_w1[:, a, :]] for a in range(2)]
+        dn_plane = [held(f"dn_plane{c}", [P, PASS], U8)[:] for c in range(2)]
+        dn_w = [[held(f"dn_w{a}_{c}", [P, PASS], U32)[:] for c in range(2)] for a in range(2)]
 
         def gather_words(a, h):
             nc.vector.tensor_copy(v_w[a][h], tab_w[a][:].bitcast(U32).indirect(half_list[h]))
 
-        def order_words(a, c):
+        def gather_quarter(a, h, s):
+            q = 2 * h + s
             nc.vector.tensor_copy(
+                v_w[a][h][:, s * QUARTER : (s + 1) * QUARTER],
+                tab_w[a][:].bitcast(U32).indirect(offsets[:, q * QUARTER // PER_COLUMN : (q + 1) * QUARTER // PER_COLUMN]),
+            )
+
+        def order_words_scalar(a, c):
+            nc.scalar.copy(
                 out=dn_w[a][c].rearrange("p (t m) -> p m t", t=PACK),
+                in_=dn_raw[a][c].bitcast(U32).rearrange("p (m t) -> p m t", t=PACK),
+            )
+
+        def order_words_vector(a, c):
+            nc.vector.tensor_copy(
+                out=dn_w[a][c].bitcast(I32).rearrange("p (t m) -> p m t", t=PACK),
                 in_=dn_raw[a][c].rearrange("p (m t) -> p m t", t=PACK),
             )
 
-        def order_second():
+        def order_plane(c):
             nc.vector.tensor_copy(
-                out=dn_w1[:].rearrange("p a (t m) -> p a m t", t=PACK),
-                in_=dn_raw1[:].rearrange("p a (m t) -> p a m t", t=PACK),
-            )
-
-        def order_planes():
-            nc.vector.tensor_copy(
-                out=dn_planes[:].rearrange("p (c t m) -> p c t m", c=2, t=PACK),
-                in_=dn_plane_raw[:].rearrange("p (c m t) -> p c t m", c=2, t=PACK),
+                out=dn_plane[c].rearrange("p (t m) -> p t m", t=PACK),
+                in_=dn_plane_raw[:, c * PASS : (c + 1) * PASS].rearrange("p (m t) -> p t m", t=PACK),
             )
 
         y = [[psum_y.tile([P, HALF], F32, name=f"y{h}_{m}") for m in range(2)] for h in range(2)]
@@ -170,33 +169,31 @@ def tile_list_xcross_mix_relu_kernel(
 
         gather_scales()
         shift(sync)
-        scale_rows(sync, wb4_plane, wb4_scales, 2)
-        load_up(sync, 0)
-        scale_rows(sync, wb4_plane, wb4_scales, 3)
-        load_up(sync, 1)
         scale_rows(sync, wb8_plane, wb8_scales, 0)
         scale_rows(sync, wb8_plane, wb8_scales, 1)
         scale_rows(sync, wb8_plane, wb8_scales, 2)
+        load_up(sync, 1)
+        load_x0(sync, 0)
+        load_wb8(sync)
         scale_rows(sync, wb8_plane, wb8_scales, 3)
         load_wb4(sync)
-        load_wb8(sync)
-        load_x0(sync, 0)
-        load_bias(sync)
         load_x0(sync, 1)
+        load_bias(sync)
         gather_words(0, 0)
-        order_words(0, 0)
-        order_planes()
+        order_words_scalar(0, 0)
+        order_plane(0)
+        order_plane(1)
         gather_words(0, 1)
-        gather_words(1, 0)
-        order_words(1, 0)
+        order_words_scalar(1, 0)
+        gather_quarter(1, 0, 0)
+        gather_quarter(1, 0, 1)
         gather_words(1, 1)
-        order_second()
-
+        order_words_scalar(0, 1)
 
         bias1 = held("bias1", [P, 2], F32)
-        nc.scalar.activation(bias1[:], bias[:], ACT.Copy, bias=1.0)
+        nc.gpsimd.tensor_scalar(bias1[:], bias[:], 1.0, 1.0, ALU.mult, ALU.add)
 
-        def hs_passes(bank, a, c, h, s):
+        def hs_passes(bank, a, c, h, s, first):
             j0 = h * HALF + s * QUARTER
             for t in range(PACK):
                 nc.tensor.matmul_mx(
@@ -205,8 +202,8 @@ def tile_list_xcross_mix_relu_kernel(
                     lhsT_scale=dn_plane[c][ROWS * a :, t * P : (t + 1) * P],
                     rhs=v_w[a][h][:, s * QUARTER : (s + 1) * QUARTER].bitcast(FP8X4),
                     rhs_scale=v_plane[ROWS * a :, j0 : j0 + QUARTER],
-                    start=(a == 0 and t == 0),
-                    stop=(a == 1 and t == PACK - 1),
+                    start=(first and t == 0),
+                    stop=(not first and t == PACK - 1),
                 )
 
         h_bf = {}
@@ -217,16 +214,15 @@ def tile_list_xcross_mix_relu_kernel(
                 for s in range(2):
                     banks[c, h, s] = psum_h.tile([P, PACK, QUARTER], F32, name="hs")
 
-        def first_passes(c):
-            for h in range(2):
-                for s in range(2):
-                    hs_passes(banks[c, h, s], 0, c, h, s)
-
-        def relu_half(c, h, passes, after=None):
-            h_bf[c, h] = held(f"h_bf{c}_{h}", [P, HALF, PACK], BF16, after=after)
+        def relu_half(c, h, ahead=()):
+            h_bf[c, h] = held(f"h_bf{c}_{h}", [P, HALF, PACK], BF16)
             for s in range(2):
-                for a in passes:
-                    hs_passes(banks[c, h, s], a, c, h, s)
+                if (h, s) in ahead:
+                    hs_passes(banks[c, h, s], 1, c, h, s, False)
+                else:
+                    opening = 0 if (c, h, s) == (1, 0, 0) else 1
+                    hs_passes(banks[c, h, s], opening, c, h, s, True)
+                    hs_passes(banks[c, h, s], 1 - opening, c, h, s, False)
                 nc.scalar.activation(
                     h_bf[c, h][:, s * QUARTER : (s + 1) * QUARTER, :],
                     banks[c, h, s][:].rearrange("p t j -> p j t"),
@@ -243,23 +239,19 @@ def tile_list_xcross_mix_relu_kernel(
                 out=h_w[c, h][:].bitcast(FP8X4), scales=h_plane[c, h][:], in_=h_bf[c, h][:].rearrange("p j t -> p (j t)")
             )
 
-        up_bf = held("up_bf", [P, 2, N, PACK], BF16)
-        up_words = held("up_words", [P, 2, N], U32)
-        up_planes = held("up_planes", [P, 2, N], U8)
-        up_w = [up_words[:, c, :] for c in range(2)]
-        up_plane = [up_planes[:, c, :] for c in range(2)]
+        up_bf = [held(f"up_bf{c}", [P, N, PACK], BF16) for c in range(2)]
+        up_w = [held("up_w0", [P, N], U32, after=("dn_raw1_1", 0))[:], held("up_w1", [P, N], U32)[:]]
+        up_plane = [held(f"up_plane{c}", [P, N], U8)[:] for c in range(2)]
 
         def round_up(c):
             nc.vector.tensor_copy(
-                up_bf[:, c, :, :].rearrange("p (n i) t -> p n t i", i=4),
+                up_bf[c][:].rearrange("p (n i) t -> p n t i", i=4),
                 up_raw[c][:].rearrange("p t (n i) -> p n t i", i=4),
             )
 
-        def quantize_up():
+        def quantize_up(c):
             nc.vector.quantize_mx(
-                out=up_words[:].rearrange("p c n -> p (c n)").bitcast(FP8X4),
-                scales=up_planes[:].rearrange("p c n -> p (c n)"),
-                in_=up_bf[:].rearrange("p c n t -> p (c n t)"),
+                out=up_w[c].bitcast(FP8X4), scales=up_plane[c], in_=up_bf[c][:].rearrange("p n t -> p (n t)")
             )
 
         picked = {}
@@ -274,22 +266,23 @@ def tile_list_xcross_mix_relu_kernel(
             picked[m, h] = held(f"picked{m}_{h}", [P, HALF], F32, after=after)[:]
             nc.vector.tensor_copy(picked[m, h], x0[m][:].indirect(half_list[h]))
 
+        ahead = ((0, 0), (0, 1), (1, 0))
         open_banks(0)
-        first_passes(0)
-        relu_half(0, 0, (1,))
-        relu_half(0, 1, (1,))
-        open_banks(1)
-        relu_half(1, 0, (0, 1))
-        relu_half(1, 1, (0, 1))
-        quantize_h(0, 0)
+        for h, s in ahead:
+            hs_passes(banks[0, h, s], 0, 0, h, s, True)
+        relu_half(0, 0, ahead)
+        relu_half(0, 1, ahead)
         round_up(0)
+        order_words_vector(1, 1)
+        open_banks(1)
+        relu_half(1, 0)
+        relu_half(1, 1)
+        quantize_up(0)
+        quantize_h(0, 0, after=("dn_raw1_1", 1024))
         round_up(1)
-        quantize_up()
-        quantize_h(1, 0, after=("up_raw1", 1024))
-        quantize_h(0, 1, after=("up_raw1", 0))
-        gather_x0(0, 1)
-        quantize_h(1, 1, after=("up_raw1", 2048), plane_after=("bias", 0))
-
+        quantize_h(0, 1, after=("up_raw1", 1024))
+        quantize_up(1)
+        quantize_h(1, 0, after=("up_raw1", 0))
 
         def up_passes(c, first=False, last=False, halves=(0, 1)):
             for h in halves:
@@ -307,17 +300,15 @@ def tile_list_xcross_mix_relu_kernel(
         def wb4_passes(first=False, halves=(0, 1)):
             for h in halves:
                 for m in range(2):
-                    for s in range(2):
-                        j0 = h * HALF + s * QUARTER
-                        nc.tensor.matmul_mx(
-                            out=y[h][m][:, s * QUARTER : (s + 1) * QUARTER],
-                            lhsT=wb4_w[:, 2 * m * P : 2 * (m + 1) * P].bitcast(FP4X4),
-                            lhsT_scale=wb4_plane[:, m * P : (m + 1) * P],
-                            rhs=v_w[1][h][:, s * QUARTER : (s + 1) * QUARTER].bitcast(FP8X4),
-                            rhs_scale=v1_plane[:, j0 : j0 + QUARTER],
-                            start=(first and s == 0),
-                            stop=False,
-                        )
+                    nc.tensor.matmul_mx(
+                        out=y[h][m][:],
+                        lhsT=wb4_w[:, 2 * m * P : 2 * (m + 1) * P].bitcast(FP4X4),
+                        lhsT_scale=wb4_plane[:, m * P : (m + 1) * P],
+                        rhs=v_w[1][h].bitcast(FP8X4),
+                        rhs_scale=v1_plane[:, h * HALF : (h + 1) * HALF],
+                        start=first,
+                        stop=False,
+                    )
 
         def wb8_passes(first=False, halves=(0, 1)):
             for h in halves:
@@ -332,12 +323,15 @@ def tile_list_xcross_mix_relu_kernel(
                         stop=False,
                     )
 
-        wb4_passes(first=True, halves=(0,))
+        gather_x0(0, 1)
+        gather_x0(1, 1)
+        quantize_h(1, 1, plane_after=("bias", 0))
+        up_passes(0, first=True, halves=(0,))
         wb8_passes(halves=(0,))
-        up_passes(0, halves=(0,))
+        wb4_passes(halves=(0,))
         up_passes(1, last=True, halves=(0,))
-        wb8_passes(first=True, halves=(1,))
-        wb4_passes(halves=(1,))
+        wb4_passes(first=True, halves=(1,))
+        wb8_passes(halves=(1,))
         up_passes(0, halves=(1,))
         up_passes(1, last=True, halves=(1,))
 
@@ -355,5 +349,5 @@ def tile_list_xcross_mix_relu_kernel(
 
         finish(0, 0)
         finish(1, 0)
-        finish(1, 1)
+        finish(1, 1, after=("biased0_0", 0))
         finish(0, 1, after=("biased1_0", 0))

@@ -81,7 +81,6 @@ def tile_list_xcross_mix_relu_kernel(
         wb4_w = held("wb4_w", [P, 2 * N], U8)
         up_raw = [held(f"up_raw{c}", [P, PACK, N], F32) for c in range(2)]
         bias = held("bias", [P, 2], F32)
-        place["end"] = place["bias"] + HALF
         v_plane = held("v_plane", [P, J], U8)
 
         def load_up(queue, c):
@@ -169,16 +168,16 @@ def tile_list_xcross_mix_relu_kernel(
 
         gather_scales()
         shift(sync)
+        load_bias(sync)
         scale_rows(sync, wb8_plane, wb8_scales, 0)
         scale_rows(sync, wb8_plane, wb8_scales, 1)
-        scale_rows(sync, wb8_plane, wb8_scales, 2)
         load_up(sync, 1)
         load_x0(sync, 0)
-        load_wb8(sync)
+        scale_rows(sync, wb8_plane, wb8_scales, 2)
         scale_rows(sync, wb8_plane, wb8_scales, 3)
+        load_wb8(sync)
         load_wb4(sync)
         load_x0(sync, 1)
-        load_bias(sync)
         gather_words(0, 0)
         order_words_scalar(0, 0)
         order_plane(0)
@@ -323,14 +322,13 @@ def tile_list_xcross_mix_relu_kernel(
                         stop=False,
                     )
 
-        gather_x0(0, 1)
-        gather_x0(1, 1)
-        quantize_h(1, 1, plane_after=("bias", 0))
+        gather_x0_whole(0)
         up_passes(0, first=True, halves=(0,))
         wb8_passes(halves=(0,))
         wb4_passes(halves=(0,))
-        up_passes(1, last=True, halves=(0,))
         wb4_passes(first=True, halves=(1,))
+        quantize_h(1, 1, plane_after=("wb4_w", 0))
+        up_passes(1, last=True, halves=(0,))
         wb8_passes(halves=(1,))
         up_passes(0, halves=(1,))
         up_passes(1, last=True, halves=(1,))
@@ -349,5 +347,5 @@ def tile_list_xcross_mix_relu_kernel(
 
         finish(0, 0)
         finish(1, 0)
-        finish(1, 1, after=("biased0_0", 0))
-        finish(0, 1, after=("biased1_0", 0))
+        finish(0, 1)
+        finish(1, 1)

@@ -81,6 +81,7 @@ def tile_list_xcross_mix_relu_kernel(
         wb4_w = held("wb4_w", [P, 2 * N], U8)
         up_raw = [held(f"up_raw{c}", [P, PACK, N], F32) for c in range(2)]
         bias = held("bias", [P, 2], F32)
+        place["end"] = place["bias"] + HALF
         v_plane = held("v_plane", [P, J], U8)
 
         def load_up(queue, c):
@@ -168,12 +169,12 @@ def tile_list_xcross_mix_relu_kernel(
 
         gather_scales()
         shift(sync)
-        load_bias(sync)
         scale_rows(sync, wb8_plane, wb8_scales, 0)
         scale_rows(sync, wb8_plane, wb8_scales, 1)
-        load_up(sync, 1)
-        load_x0(sync, 0)
         scale_rows(sync, wb8_plane, wb8_scales, 2)
+        load_up(sync, 1)
+        load_bias(sync)
+        load_x0(sync, 0)
         scale_rows(sync, wb8_plane, wb8_scales, 3)
         load_wb8(sync)
         load_wb4(sync)
@@ -239,7 +240,7 @@ def tile_list_xcross_mix_relu_kernel(
             )
 
         up_bf = [held(f"up_bf{c}", [P, N, PACK], BF16) for c in range(2)]
-        up_w = [held("up_w0", [P, N], U32, after=("dn_raw1_1", 0))[:], held("up_w1", [P, N], U32)[:]]
+        up_w = [held("up_w0", [P, N], U32)[:], held("up_w1", [P, N], U32)[:]]
         up_plane = [held(f"up_plane{c}", [P, N], U8)[:] for c in range(2)]
 
         def round_up(c):
@@ -277,9 +278,9 @@ def tile_list_xcross_mix_relu_kernel(
         relu_half(1, 0)
         relu_half(1, 1)
         quantize_up(0)
-        quantize_h(0, 0, after=("dn_raw1_1", 1024))
+        quantize_h(0, 0, after=("up_raw0", 0))
         round_up(1)
-        quantize_h(0, 1, after=("up_raw1", 1024))
+        quantize_h(0, 1, plane_after=("bias", 0))
         quantize_up(1)
         quantize_h(1, 0, after=("up_raw1", 0))
 

@@ -168,13 +168,13 @@ def tile_list_xcross_mix_relu_kernel(
             nc.vector.tensor_copy(v_plane[:], tab_plane[:].indirect(offsets[:]))
 
         gather_scales()
-        shift(sync)
         scale_rows(sync, wb8_plane, wb8_scales, 0)
         scale_rows(sync, wb8_plane, wb8_scales, 1)
         scale_rows(sync, wb8_plane, wb8_scales, 2)
         load_up(sync, 1)
         load_bias(sync)
         load_x0(sync, 0)
+        shift(sync)
         scale_rows(sync, wb8_plane, wb8_scales, 3)
         load_wb8(sync)
         load_wb4(sync)

import math
from contextlib import ExitStack

import concourse.mybir as mybir

K, R, N, T, J = 1024, 1024, 256, 1024, 512
FLOPS = 2 * J * (K * R + K * N + R * N)

F32 = mybir.dt.float32
BF16 = mybir.dt.bfloat16
I32 = mybir.dt.int32
U32 = mybir.dt.uint32
U16 = mybir.dt.uint16
U8 = mybir.dt.uint8
FP8X4 = mybir.dt.float8_e4m3fn_x4
FP4X4 = mybir.dt.float4_e2m1fn_x4
ACT = mybir.ActivationFunctionType
ALU = mybir.AluOpType

P = 128
PACK = 4
PASS = P * PACK
GROUP = 8
QUADRANT = 32
QUADS = P // QUADRANT
ROWS = QUADRANT // GROUP
PER_COLUMN = 16
HALF = J // 2
QUARTER = J // 4
SHIFT_ROWS = 112


def tile_list_xcross_mix_relu_kernel(
    tc, tab_words, tab_scales, wb8_words, wb8_scales, wb4_words, wb4_scales, dn_words, dn_scales, upw, x0T, b, offs, out
):
    nc = tc.nc
    with ExitStack() as ctx:
        lists = ctx.enter_context(tc.tile_pool(name="lists", bufs=1))
        keep = ctx.enter_context(tc.tile_pool(name="keep", bufs=1))
        psum_h = ctx.enter_context(tc.psum_pool(name="psum_h", bufs=4))
        psum_y = ctx.enter_context(tc.psum_pool(name="psum_y", bufs=1))

        place = {"end": 0}
        width = {F32: 4, I32: 4, U32: 4, BF16: 2, U8: 1}

        def held(name, shape, dtype, after=None):
            if after is None:
                place[name] = place["end"]
                place["end"] = place["end"] + math.prod(shape[1:]) * width[dtype] + 63 & -64
            else:
                place[name] = place[after[0]] + after[1]
            return keep.tile(shape, dtype, name=name, align_bytes=64, offset=place[name])

        offsets = lists.tile([P, J // PER_COLUMN], U16, name="offsets")
        half_list = [offsets[:, h * HALF // PER_COLUMN : (h + 1) * HALF // PER_COLUMN] for h in range(2)]

        tab_plane = held("tab_plane", [P, T], U8)
        dn_plane_raw = held("dn_plane_raw", [P, R], U8)
        late_planes = held("late_planes", [P, 2 * N + J], U8)
        wb8_plane = late_planes[:, 0:N]
        wb4_plane = late_planes[:, N : 2 * N]
        v1_plane = late_planes[:, 2 * N : 2 * N + J]
        nc.vector.memset(tab_plane[:].bitcast(I32), 0)
        nc.vector.memset(dn_plane_raw[:].bitcast(I32), 0)
        nc.vector.memset(late_planes[:].bitcast(I32), 0)

        def scale_rows(queue, plane, scales, quad):
            passes = scales.shape[0]
            queue.dma_start(
                out=plane[QUADRANT * quad : QUADRANT * quad + ROWS * passes, :].bitcast(I32),
                in_=scales[:, ROWS * quad : ROWS * (quad + 1), :].bitcast(I32),
            )

        def words_of(words, a):
            return words[a].rearrange("p c i -> p (c i)").bitcast(I32)

        tab_w = [held(f"tab_w{a}", [P, T], I32) for a in range(2)]
        dn_raw = [[held(f"dn_raw{a}_{c}", [P, PASS], I32)[:] for c in range(2)] for a in range(2)]
        x0 = [held(f"x0_{m}", [P, T], F32) for m in range(2)]
        wb8_w = held("wb8_w", [P, N], I32)
        wb4_w = held("wb4_w", [P, 2 * N], U8)
        up_raw = [held(f"up_raw{c}", [P, PACK, N], F32) for c in range(2)]
        bias = held("bias", [P, 2], F32)
        place["end"] = place["bias"] + HALF
        v_plane = held("v_plane", [P, J], U8)

        def load_up(queue, c):
            queue.dma_start(out=up_raw[c][:], in_=upw[c * PASS : (c + 1) * PASS, :].rearrange("(p t) n -> p t n", t=PACK))

        def load_bias(queue):
            with nc.allow_non_contiguous_dma(reason="one bias value a partition"):
                queue.dma_start(out=bias[:], in_=b.rearrange("(m p) -> p m", p=P))

        def shift(queue):
            queue.dma_start(out=v1_plane[0:SHIFT_ROWS, :].bitcast(I32), in_=v_plane[ROWS : ROWS + SHIFT_ROWS, :].bitcast(I32))

        def load_tab(queue, a):
            queue.dma_start(out=tab_w[a][:], in_=words_of(tab_words, a))

        def load_dn(queue, a, c):
            queue.dma_start(out=dn_raw[a][c], in_=words_of(dn_words, a)[:, c * PASS : (c + 1) * PASS])

        def load_x0(queue, m):
            queue.dma_start(out=x0[m][:], in_=x0T[m * P : (m + 1) * P, :])

        def load_wb8(queue):
            queue.dma_start(out=wb8_w[:], in_=words_of(wb8_words, 0))

        def load_wb4(queue):
            queue.dma_start(out=wb4_w[:].bitcast(I32), in_=wb4_words[0].bitcast(I32))

        sync, scalar, pool = nc.sync, nc.scalar, nc.gpsimd
        sync.dma_start(offsets[:], offs)
        scale_rows(scalar, tab_plane, tab_scales, 0)
        scale_rows(sync, tab_plane, tab_scales, 2)
        scale_rows(scalar, tab_plane, tab_scales, 1)
        scale_rows(sync, tab_plane, tab_scales, 3)
        load_tab(sync, 0)
        scale_rows(sync, dn_plane_raw, dn_scales, 0)
        load_dn(sync, 0, 0)
        scale_rows(sync, dn_plane_raw, dn_scales, 1)
        scale_rows(sync, dn_plane_raw, dn_scales, 2)
        scale_rows(sync, dn_plane_raw, dn_scales, 3)
        load_dn(sync, 1, 0)
        load_tab(sync, 1)
        load_dn(sync, 0, 1)
        load_up(sync, 0)
        load_dn(sync, 1, 1)
        for quad in range(QUADS):
            scale_rows(pool, wb4_plane, wb4_scales, quad)

        v_after = {(0, 1): ("dn_plane_raw", 0)}
        v_w = [[held(f"v_w{a}_{h}", [P, HALF], U32, after=v_after.get((a, h)))[:] for h in range(2)] for a in range(2)]
        dn_plane = [held(f"dn_plane{c}", [P, PASS], U8)[:] for c in range(2)]
        dn_w = [[held(f"dn_w{a}_{c}", [P, PASS], U32)[:] for c in range(2)] for a in range(2)]

        def gather_words(a, h):
            nc.vector.tensor_copy(v_w[a][h], tab_w[a][:].bitcast(U32).indirect(half_list[h]))

        def gather_quarter(a, h, s):
            q = 2 * h + s
            nc.vector.tensor_copy(
                v_w[a][h][:, s * QUARTER : (s + 1) * QUARTER],
                tab_w[a][:].bitcast(U32).indirect(offsets[:, q * QUARTER // PER_COLUMN : (q + 1) * QUARTER // PER_COLUMN]),
            )

        def order_words_scalar(a, c):
            nc.scalar.copy(
                out=dn_w[a][c].rearrange("p (t m) -> p m t", t=PACK),
                in_=dn_raw[a][c].bitcast(U32).rearrange("p (m t) -> p m t", t=PACK),
            )

        def order_words_vector(a, c):
            nc.vector.tensor_copy(
                out=dn_w[a][c].bitcast(I32).rearrange("p (t m) -> p m t", t=PACK),
                in_=dn_raw[a][c].rearrange("p (m t) -> p m t", t=PACK),
            )

        def order_plane(c):
            nc.vector.tensor_copy(
                out=dn_plane[c].rearrange("p (t m) -> p t m", t=PACK),
                in_=dn_plane_raw[:, c * PASS : (c + 1) * PASS].rearrange("p (m t) -> p t m", t=PACK),
            )

        y = [[psum_y.tile([P, HALF], F32, name=f"y{h}_{m}") for m in range(2)] for h in range(2)]

        def gather_scales():
            nc.vector.tensor_copy(v_plane[:], tab_plane[:].indirect(offsets[:]))

        gather_scales()
        scale_rows(sync, wb8_plane, wb8_scales, 0)
        scale_rows(sync, wb8_plane, wb8_scales, 1)
        scale_rows(sync, wb8_plane, wb8_scales, 2)
        load_up(sync, 1)
        load_bias(sync)
        load_x0(sync, 0)
        shift(sync)
        scale_rows(sync, wb8_plane, wb8_scales, 3)
        load_wb8(sync)
        load_wb4(sync)
        load_x0(sync, 1)
        gather_words(0, 0)
        order_words_scalar(0, 0)
        order_plane(0)
        order_plane(1)
        gather_words(0, 1)
        order_words_scalar(1, 0)
        gather_quarter(1, 0, 0)
        gather_quarter(1, 0, 1)
        gather_words(1, 1)
        order_words_scalar(0, 1)

        bias1 = held("bias1", [P, 2], F32)
        nc.gpsimd.tensor_scalar(bias1[:], bias[:], 1.0, 1.0, ALU.mult, ALU.add)

        def hs_passes(bank, a, c, h, s, first):
            j0 = h * HALF + s * QUARTER
            for t in range(PACK):
                nc.tensor.matmul_mx(
                    out=bank[:, t, :],
                    lhsT=dn_w[a][c][:, t * P : (t + 1) * P].bitcast(FP8X4),
                    lhsT_scale=dn_plane[c][ROWS * a :, t * P : (t + 1) * P],
                    rhs=v_w[a][h][:, s * QUARTER : (s + 1) * QUARTER].bitcast(FP8X4),
                    rhs_scale=v_plane[ROWS * a :, j0 : j0 + QUARTER],
                    start=(first and t == 0),
                    stop=(not first and t == PACK - 1),
                )

        h_bf = {}
        banks = {}

        def open_banks(c):
            for h in range(2):
                for s in range(2):
                    banks[c, h, s] = psum_h.tile([P, PACK, QUARTER], F32, name="hs")

        def relu_half(c, h, ahead=()):
            h_bf[c, h] = held(f"h_bf{c}_{h}", [P, HALF, PACK], BF16)
            for s in range(2):
                if (h, s) in ahead:
                    hs_passes(banks[c, h, s], 1, c, h, s, False)
                else:
                    opening = 0 if (c, h, s) == (1, 0, 0) else 1
                    hs_passes(banks[c, h, s], opening, c, h, s, True)
                    hs_passes(banks[c, h, s], 1 - opening, c, h, s, False)
                nc.scalar.activation(
                    h_bf[c, h][:, s * QUARTER : (s + 1) * QUARTER, :],
                    banks[c, h, s][:].rearrange("p t j -> p j t"),
                    ACT.Relu,
                )

        h_w = {}
        h_plane = {}

        def quantize_h(c, h, after=None, plane_after=None):
            h_w[c, h] = held(f"h_w{c}_{h}", [P, HALF], U32, after=after)
            h_plane[c, h] = held(f"h_plane{c}_{h}", [P, HALF], U8, after=plane_after)
            nc.vector.quantize_mx(
                out=h_w[c, h][:].bitcast(FP8X4), scales=h_plane[c, h][:], in_=h_bf[c, h][:].rearrange("p j t -> p (j t)")
            )

        up_bf = [held(f"up_bf{c}", [P, N, PACK], BF16) for c in range(2)]
        up_w = [held("up_w0", [P, N], U32)[:], held("up_w1", [P, N], U32)[:]]
        up_plane = [held(f"up_plane{c}", [P, N], U8)[:] for c in range(2)]

        def round_up(c):
            nc.vector.tensor_copy(
                up_bf[c][:].rearrange("p (n i) t -> p n t i", i=4),
                up_raw[c][:].rearrange("p t (n i) -> p n t i", i=4),
            )

        def quantize_up(c):
            nc.vector.quantize_mx(
                out=up_w[c].bitcast(FP8X4), scales=up_plane[c], in_=up_bf[c][:].rearrange("p n t -> p (n t)")
            )

        picked = {}

        def gather_x0_whole(m, after=None):
            both = held(f"picked{m}", [P, J], F32, after=after)
            nc.vector.tensor_copy(both[:], x0[m][:].indirect(offsets[:]))
            for h in range(2):
                picked[m, h] = both[:, h * HALF : (h + 1) * HALF]

        def gather_x0(m, h, after=None):
            picked[m, h] = held(f"picked{m}_{h}", [P, HALF], F32, after=after)[:]
            nc.vector.tensor_copy(picked[m, h], x0[m][:].indirect(half_list[h]))

        ahead = ((0, 0), (0, 1), (1, 0))
        open_banks(0)
        for h, s in ahead:
            hs_passes(banks[0, h, s], 0, 0, h, s, True)
        relu_half(0, 0, ahead)
        relu_half(0, 1, ahead)
        round_up(0)
        order_words_vector(1, 1)
        open_banks(1)
        relu_half(1, 0)
        relu_half(1, 1)
        quantize_up(0)
        quantize_h(0, 0, after=("up_raw0", 0))
        round_up(1)
        quantize_h(0, 1, plane_after=("bias", 0))
        quantize_up(1)
        quantize_h(1, 0, after=("up_raw1", 0))

        def up_passes(c, first=False, last=False, halves=(0, 1)):
            for h in halves:
                for m in (h, 1 - h):
                    nc.tensor.matmul_mx(
                        out=y[h][m][:],
                        lhsT=up_w[c][:, m * P : (m + 1) * P].bitcast(FP8X4),
                        lhsT_scale=up_plane[c][:, m * P : (m + 1) * P],
                        rhs=h_w[c, h][:].bitcast(FP8X4),
                        rhs_scale=h_plane[c, h][:],
                        start=first,
                        stop=last,
                    )

        def wb4_passes(first=False, halves=(0, 1)):
            for h in halves:
                for m in range(2):
                    nc.tensor.matmul_mx(
                        out=y[h][m][:],
                        lhsT=wb4_w[:, 2 * m * P : 2 * (m + 1) * P].bitcast(FP4X4),
                        lhsT_scale=wb4_plane[:, m * P : (m + 1) * P],
                        rhs=v_w[1][h].bitcast(FP8X4),
                        rhs_scale=v1_plane[:, h * HALF : (h + 1) * HALF],
                        start=first,
                        stop=False,
                    )

        def wb8_passes(first=False, halves=(0, 1)):
            for h in halves:
                for m in range(2):
                    nc.tensor.matmul_mx(
                        out=y[h][m][:],
                        lhsT=wb8_w[:, m * P : (m + 1) * P].bitcast(FP8X4),
                        lhsT_scale=wb8_plane[:, m * P : (m + 1) * P],
                        rhs=v_w[0][h].bitcast(FP8X4),
                        rhs_scale=v_plane[:, h * HALF : (h + 1) * HALF],
                        start=first,
                        stop=False,
                    )

        gather_x0_whole(0)
        up_passes(0, first=True, halves=(0,))
        wb8_passes(halves=(0,))
        wb4_passes(halves=(0,))
        wb4_passes(first=True, halves=(1,))
        quantize_h(1, 1, plane_after=("wb4_w", 0))
        up_passes(1, last=True, halves=(0,))
        wb8_passes(halves=(1,))
        up_passes(0, halves=(1,))
        up_passes(1, last=True, halves=(1,))

        def finish(m, h, after=None, queue=nc.sync):
            res = held(f"res{m}_{h}", [P, HALF], F32, after=after)
            if (m, h) in picked:
                nc.vector.scalar_tensor_tensor(
                    out=res[:], in0=y[h][m][:], scalar=bias1[:, m : m + 1], in1=picked[m, h], op0=ALU.add, op1=ALU.mult
                )
            else:
                biased = held(f"biased{m}_{h}", [P, HALF], F32)
                nc.scalar.activation(biased[:], y[h][m][:], ACT.Identity, bias=bias1[:, m : m + 1])
                nc.vector.tensor_tensor(res[:], x0[m][:].indirect(half_list[h]), biased[:], ALU.mult)
            queue.dma_start(out=out[m * P : (m + 1) * P, h * HALF : (h + 1) * HALF], in_=res[:])

        finish(0, 0)
        finish(1, 0)
        finish(0, 1)
        finish(1, 1)
